import numpy as np
import ml_dtypes


def mxq(x, axis, fmt="e4m3"):
    dtype, down = {"e4m3": (ml_dtypes.float8_e4m3fn, 7), "e5m2": (ml_dtypes.float8_e5m2, 14)}[fmt]
    v = np.moveaxis(np.asarray(x, np.float32).astype(ml_dtypes.bfloat16).astype(np.float64), axis, -1)
    blocks = v.reshape(v.shape[:-1] + (-1, 32))
    amax = np.abs(blocks).max(-1, keepdims=True)
    byte = np.maximum(np.where(amax > 0, np.frexp(amax)[1] - 1 + 127, 0) - down, 1)
    scale = np.exp2(byte - 127.0)
    codes = (blocks / scale).astype(np.float32).astype(dtype).astype(np.float64)
    return np.moveaxis((codes * scale).reshape(v.shape), -1, axis)


WIDE = False


def mx_kscale(k):
    if not WIDE:
        return np.ones(k)
    levels = np.array([10, -10, 5, -5, 0])
    if k % 512:
        return np.exp2(np.random.permutation(np.resize(levels, k // 32))).repeat(32)
    a = np.empty((k // 512, 16))
    for p in range(k // 512):
        a[p, :8] = np.random.permutation(np.resize(levels, 8))
        for g in range(8):
            far = levels[np.abs(levels - a[p, g]) >= 10]
            a[p, g + 8] = far[np.random.randint(len(far))]
    return np.exp2(a.ravel()).repeat(32)


def f64(x):
    return np.asarray(x).astype(np.float64)


def striped(idx):
    return np.tile(idx.reshape(-1, 16).T, (8, 1)).astype(np.uint16)


def unstriped(offs):
    return offs[:16].T.reshape(-1).astype(np.int64)


def striped8(idx):
    return np.concatenate([x.reshape(-1, 16).T for x in idx]).astype(np.uint16)


def runs(offs, k):
    lists = np.stack([offs[16 * r : 16 * r + 16].T.reshape(-1) for r in range(8)]).astype(np.int64)
    return lists[np.arange(k) % 512 // 64]


def pack_weight(w):
    k, n = w.shape
    w = f64(np.asarray(w, np.float32).astype(ml_dtypes.bfloat16)).reshape(k // 32, 32, n)
    amax = np.abs(w).max(1)
    byte = np.clip(np.where(amax > 0, np.frexp(amax)[1] - 1 + 127 - 7, 1), 1, 254)
    scaled = (w * np.exp2(127.0 - byte)[:, None, :]).reshape(k, n).astype(np.float32)
    words = np.ascontiguousarray(scaled.reshape(k // 512, 128, 4, n).transpose(0, 1, 3, 2)).astype(ml_dtypes.float8_e4m3fn).view(np.uint8)
    return words, np.ascontiguousarray(byte.astype(np.uint8).reshape(k // 512, 16, n))


def unpack_weight(words, scales):
    g, p, n, _ = words.shape
    vals = np.ascontiguousarray(words).view(ml_dtypes.float8_e4m3fn).astype(np.float64) * np.repeat(np.exp2(scales.astype(np.float64) - 127.0), 8, axis=1)[..., None]
    return vals.transpose(0, 1, 3, 2).reshape(g * 512, n)


K, T, S, H, C, G = 512, 1024, 512, 512, 512, 2048


def setup_inputs():
    n = np.random.standard_normal
    s = mx_kscale(K)[:, None]
    packed_xT = pack_weight(n((K, T)) * s)
    packed_dT = pack_weight(n((K, G)) / s)
    return {
        "x_words": packed_xT[0],
        "x_scales": packed_xT[1],
        "w1": (n((K, H)) / np.sqrt(K) / s).astype(np.float32),
        "gs": (np.random.uniform(0.5, 1.5, (K, 1)) / s).astype(np.float32),
        "gk": (np.random.uniform(0.5, 1.5, (K, 1)) * s).astype(np.float32),
        "d_words": packed_dT[0],
        "d_scales": packed_dT[1],
        "offs": striped(np.random.permutation(T)[:S]),
        "n1": striped(np.random.permutation(S)),
        "n2": striped(np.random.permutation(S)),
        "n3": striped(np.random.permutation(S)),
        "n4": striped(np.random.permutation(S)),
        "n5": striped8(np.stack([np.random.permutation(S) for _ in range(8)])),
        "n6": striped8(np.stack([np.random.permutation(S) for _ in range(8)])),
        "n7": striped8(np.stack([np.random.permutation(S) for _ in range(8)])),
        "cand": striped(np.random.permutation(T)[:C]),
        "k1": striped8(np.random.randint(0, G, (8, H))),
        "n8": striped8(np.stack([np.random.permutation(S) for _ in range(8)])),
        "n9": striped8(np.stack([np.random.permutation(S) for _ in range(8)])),
    }


def reference(x_words, x_scales, w1, gs, gk, d_words, d_scales, offs, n1, n2, n3, n4, n5, n6, n7, cand, k1, n8, n9):
    x_cand = unpack_weight(x_words, x_scales)[:, unstriped(cand)]
    xq = unpack_weight(x_words, x_scales)[:, unstriped(offs)]
    y = mxq(f64(w1), 0, "e4m3").T @ xq
    z = f64(gs) * (0.75 * (y[:, unstriped(n1)] * y[:, unstriped(n2)] - (y[:, unstriped(n3)] * y[:, unstriped(n4)])))
    a = 0.0625 * ((x_cand.T @ mxq(z, 0, "e4m3")))
    d_k1 = unpack_weight(d_words, d_scales)[np.arange(K)[:, None], runs(k1, K)]
    z2 = f64(gk) * (y + y[np.arange(H)[:, None], runs(n5, H)] - (np.maximum(y[np.arange(H)[:, None], runs(n6, H)], y[np.arange(H)[:, None], runs(n7, H)])))
    b = 0.0625 * ((d_k1.T @ mxq(z2, 0, "e4m3")))
    return (a - (a[np.arange(C)[:, None], runs(n8, C)])) / (np.abs(b) + np.abs(b[np.arange(H)[:, None], runs(n9, H)]) + 0.5)

@@ -1,0 +1,252 @@
+from contextlib import ExitStack
+
+import concourse.mybir as mybir
+from concourse.masks import make_identity
+
+K, T, S, G = 512, 1024, 512, 2048
+FLOPS = 3 * 2 * 512 * 512 * 512
+
+F32 = mybir.dt.float32
+BF16 = mybir.dt.bfloat16
+I32 = mybir.dt.int32
+U32 = mybir.dt.uint32
+U16 = mybir.dt.uint16
+U8 = mybir.dt.uint8
+FP8X4 = mybir.dt.float8_e4m3fn_x4
+ALU = mybir.AluOpType
+ACT = mybir.ActivationFunctionType
+
+P = 128
+PACK = 4
+HALF = S // 2
+LCOLS = S // 16
+
+
+def tile_picked_cdkeynormbdettrim_none_p_kernel(tc, x_words, x_scales, w1, gs, gk, d_words, d_scales, offs, n1, n2, n3, n4, n5, n6, n7, cand, k1, n8, n9, out):
+    nc = tc.nc
+    with ExitStack() as ctx:
+        lists = ctx.enter_context(tc.tile_pool(name="lists", bufs=1))
+        sb = ctx.enter_context(tc.tile_pool(name="sb", bufs=1))
+        head = ctx.enter_context(tc.tile_pool(name="head", bufs=1))
+        psum = ctx.enter_context(tc.psum_pool(name="psum", bufs=1))
+
+        def new(shape, dtype, name, tag=None):
+            return sb.tile(shape, dtype, name=name, tag=tag or name, align_bytes=64)
+
+        def after_w(shape, dtype, name, offset):
+            return head.tile(shape, dtype, name=name, align_bytes=64, offset=offset)
+
+        def load_list(src, name):
+            tile = lists.tile([P, LCOLS], U16, name=name)
+            nc.sync.dma_start(tile[:], src)
+            return tile
+
+        def halves():
+            return [(slice(h * HALF, (h + 1) * HALF), slice(h * LCOLS // 2, (h + 1) * LCOLS // 2)) for h in range(2)]
+
+        xs = new([P, T], U8, "xs")
+        nc.gpsimd.memset(xs[:].bitcast(I32), 0)
+        ds = new([P, G], U8, "ds")
+        nc.gpsimd.memset(ds[:].bitcast(I32), 0)
+        key_scales = new([P, S], U8, "key_scales")
+        nc.gpsimd.memset(key_scales[:].bitcast(I32), 0)
+        eight = new([P, 1], F32, "eight")
+        nc.gpsimd.memset(eight[:], 8.0)
+        ident = new([P, P], F32, "ident")
+        make_identity(nc, ident[:])
+        rows = [new([P, 2 * S], F32, "rows%d" % t) for t in range(PACK)]
+        for t in range(PACK):
+            nc.vector.memset(rows[t][:, S:], 0.0)
+
+        l_offs = load_list(offs, "l_offs")
+        xs_rows = x_scales[0].bitcast(I32)
+        for r in range(4):
+            nc.sync.dma_start(xs[r:P:32, :].bitcast(I32), xs_rows[r:16:4, :])
+        xw = new([P, T], U32, "xw")
+        nc.sync.dma_start(xw[:].bitcast(I32), x_words[0].rearrange("p n t -> p (n t)").bitcast(I32))
+        w_rows = w1.rearrange("(p j) c -> p j c", j=PACK)
+        w_raw = []
+        for h in range(2):
+            wr = new([P, PACK, HALF], F32, "w_raw%d" % h)
+            nc.sync.dma_start(wr[:], w_rows[:, :, h * HALF:(h + 1) * HALF])
+            w_raw.append(wr)
+        l_n6 = load_list(n6, "l_n6")
+        l_n7 = load_list(n7, "l_n7")
+        l_cand = load_list(cand, "l_cand")
+        l_n5 = load_list(n5, "l_n5")
+        dw = new([P, G], U32, "dw")
+        nc.sync.dma_start(dw[:].bitcast(I32), d_words[0].rearrange("p n t -> p (n t)").bitcast(I32))
+        l_k1 = load_list(k1, "l_k1")
+        ds_rows = d_scales[0].bitcast(I32)
+        nc.sync.dma_start(ds[0:P:8, :].bitcast(I32), ds_rows)
+        l_n1 = load_list(n1, "l_n1")
+        l_n2 = load_list(n2, "l_n2")
+        l_n3 = load_list(n3, "l_n3")
+        l_n4 = load_list(n4, "l_n4")
+        l_n9 = load_list(n9, "l_n9")
+        l_n8 = load_list(n8, "l_n8")
+
+        tok_scales = new([P, S], U8, "tok_scales")
+        nc.vector.tensor_copy(tok_scales[:], xs[:].indirect(l_offs[:]))
+        tok_words = new([P, S], U32, "tok_words")
+        nc.vector.tensor_copy(tok_words[:], xw[:].indirect(l_offs[:]))
+
+        w_bf = after_w([P, PACK, P, PACK], BF16, "w_bf", 0)
+        for q in range(4):
+            src = w_raw[q // 2][:, :, (q % 2) * P:(q % 2 + 1) * P].rearrange("p j (m t) -> p m j t", t=PACK)
+            dst = w_bf[:, :, q * 32:(q + 1) * 32, :].rearrange("p t m j -> p m j t")
+            if q < 3:
+                nc.scalar.copy(dst, src)
+            else:
+                nc.vector.tensor_copy(dst, src)
+        gk_b = new([P, K], F32, "gk_b", "w_raw0")
+        nc.sync.dma_start(gk_b[:], gk.rearrange("k o -> (k o)").partition_broadcast(P))
+        gs_b = new([P, K], F32, "gs_b", "w_raw1")
+        nc.sync.dma_start(gs_b[:], gs.rearrange("k o -> (k o)").partition_broadcast(P))
+        w_codes = new([P, S], U32, "w_codes")
+        w_scales = new([P, S], U8, "w_scales")
+        for t in range(PACK):
+            cols = slice(t * P, (t + 1) * P)
+            nc.vector.quantize_mx(out=w_codes[:, cols].bitcast(FP8X4), scales=w_scales[:, cols], in_=w_bf[:, t].rearrange("p m j -> p (m j)"))
+
+        def product(acc, t, lw, ls, rw, rs):
+            cols = slice(t * P, (t + 1) * P)
+            nc.tensor.matmul_mx(out=acc[:], lhsT=lw[:, cols].bitcast(FP8X4), lhsT_scale=ls[:, cols], rhs=rw[:].bitcast(FP8X4), rhs_scale=rs[:], start=True, stop=True)
+
+        def deal_words(dst, src):
+            nc.vector.tensor_copy(dst[:].rearrange("p (t c i) -> p c t i", t=PACK, i=4), src[:].rearrange("p (c i t) -> p c t i", t=PACK, i=4))
+
+        def deal_bytes(dst, src):
+            nc.vector.tensor_copy(dst[:].rearrange("p (t m) -> p m t", t=PACK), src[:].rearrange("p (m t) -> p m t", t=PACK))
+
+        def gather(engine, dst, window, offsets, scale=1.0):
+            if engine == "scalar":
+                nc.scalar.activation(dst, window.indirect(offsets), ACT.Copy, scale=scale)
+            else:
+                nc.vector.tensor_copy(dst, window.indirect(offsets))
+
+        def bank(kind, n, name):
+            return psum.tile([P, S], F32, name=name, tag="%s%d" % (kind, n))
+
+        def turned_sum(dst, first, second):
+            nc.tensor.matmul(dst, first, ident[:], start=True, stop=False, is_transpose=True)
+            nc.tensor.matmul(dst, second, ident[:], start=False, stop=True, is_transpose=True)
+
+        def block(n):
+            return slice(n * P, (n + 1) * P)
+
+        def quantise(name, turned, gain):
+            woven = new([P, S, PACK], BF16, name + "_bf")
+            codes = new([P, S], U32, name + "_codes")
+            scales = new([P, S], U8, name + "_scales")
+            gain_v = gain[:].rearrange("j (p t) -> j p t", t=PACK)
+            for h in range(2):
+                pairs = bank("A", h, name + "_pairs%d" % h)
+                for b2 in range(2):
+                    jb = 2 * h + b2
+                    flat = new([P, K], BF16, name + "_flat%d" % jb)
+                    nc.vector.tensor_tensor(flat[:].rearrange("j (p t) -> j p t", t=PACK), turned[jb][:].rearrange("j (t p) -> j p t", t=PACK), gain_v, ALU.mult)
+                    words = flat[:].bitcast(F32)
+                    for u in range(2):
+                        nc.tensor.transpose(pairs[:, block(2 * b2 + u)], words[:, u:2 * P:2], ident[:])
+                cols = slice(h * HALF, (h + 1) * HALF)
+                dst = woven[:, cols, :].rearrange("p c t -> p (c t)")
+                nc.scalar.copy(dst.bitcast(F32).rearrange("p (b j u) -> p b j u", b=2, u=2), pairs[:].rearrange("p (b u j) -> p b j u", b=2, u=2))
+            for h in range(2):
+                cols = slice(h * HALF, (h + 1) * HALF)
+                nc.vector.quantize_mx(out=codes[:, cols].bitcast(FP8X4), scales=scales[:, cols], in_=woven[:, cols, :].rearrange("p c t -> p (c t)"))
+            return codes, scales
+
+        ys = []
+        for t in range(PACK):
+            ys.append(bank("A", t, "y%d" % t))
+            product(ys[t], t, w_codes, w_scales, tok_words, tok_scales)
+
+        cand_words_l = after_w([P, S], U32, "cand_words_l", 0)
+        nc.vector.tensor_copy(cand_words_l[:], xw[:].indirect(l_cand[:]))
+        cand_scales_l = after_w([P, S], U8, "cand_scales_l", 2048)
+        nc.vector.tensor_copy(cand_scales_l[:], xs[:].indirect(l_cand[:]))
+        cand_words = new([P, S], U32, "cand_words")
+        deal_words(cand_words, cand_words_l)
+        cand_scales = new([P, S], U8, "cand_scales")
+        deal_bytes(cand_scales, cand_scales_l)
+        key_scales_l = after_w([P, S], U8, "key_scales_l", 2560)
+        nc.vector.tensor_copy(key_scales_l[:], ds[:].indirect(l_k1[:]))
+        key_words_l = after_w([P, S], U32, "key_words_l", 3072)
+        nc.vector.tensor_copy(key_words_l[:], dw[:].indirect(l_k1[:]))
+        key_scales_d = new([P, S], U8, "key_scales_d")
+        deal_bytes(key_scales_d, key_scales_l)
+        key_words = new([P, S], U32, "key_words")
+        deal_words(key_words, key_words_l)
+        for e in range(4):
+            first = 8 * e
+            nc.sync.dma_start(key_scales[e:P:32, :].bitcast(I32), key_scales_d[first:P:32, :].bitcast(I32))
+
+        turned = [bank("B", jb, "z2_turned%d" % jb) for jb in range(4)]
+        brows = [new([P, 2 * S], F32, "brows%d" % t) for t in range(PACK)]
+        for t in range(PACK):
+            y = rows[t]
+            nc.scalar.activation(y[:, :S], ys[t][:], ACT.Copy)
+            g6 = brows[t][:, S:]
+            g7 = new([P, S], F32, "g7_%d" % t)
+            gather("scalar", g6, y[:], l_n6[:])
+            gather("scalar", g7[:], y[:], l_n7[:])
+            m = new([P, S], F32, "m_%d" % t)
+            nc.vector.tensor_tensor(m[:], g6, g7[:], ALU.max)
+            u = new([P, S], F32, "u_%d" % t)
+            nc.vector.tensor_tensor(u[:], y[:].indirect(l_n5[:]), m[:], ALU.subtract)
+            for jb in range(4):
+                turned_sum(turned[jb][:, block(t)], y[:, block(jb)], u[:, block(jb)])
+        z2_codes, z2_scales = quantise("z2", turned, gk_b)
+
+        for t in range(PACK):
+            acc = bank("A", (t + 2) % 4, "b%d" % t)
+            product(acc, t, key_words, key_scales, z2_codes, z2_scales)
+            nc.scalar.activation(brows[t][:, :S], acc[:], ACT.Abs)
+
+        turned = [bank("B", jb, "z_turned%d" % jb) for jb in range(4)]
+        for t in range(PACK):
+            y = rows[t]
+            prods = []
+            for (la, lb, factor, nm) in ((l_n1, l_n2, 0.75, "12"), (l_n3, l_n4, -0.75, "34")):
+                g = new([P, S], F32, "g%s_%d" % (nm, t))
+                gather("scalar", g[:], y[:], la[:], factor)
+                pr = new([P, S], F32, "p%s_%d" % (nm, t), "z2_bf" if (nm, t) == ("12", 2) else None)
+                nc.vector.tensor_tensor(pr[:], y[:].indirect(lb[:]), g[:], ALU.mult)
+                prods.append(pr)
+            for jb in range(4):
+                turned_sum(turned[jb][:, block(t)], prods[0][:, block(jb)], prods[1][:, block(jb)])
+        g9 = []
+        for t in range(PACK):
+            g9.append(new([P, S], F32, "g9_%d" % t))
+            gather("scalar", g9[t][:], brows[t][:], l_n9[:])
+        z_codes, z_scales = quantise("z", turned, gs_b)
+
+        out_rows = out.rearrange("(p t) n -> t p n", t=PACK)
+        accs = []
+        for t in range(PACK):
+            accs.append(bank("A", (t + 2) % 4, "a%d" % t))
+            product(accs[t], t, cand_words, cand_scales, z_codes, z_scales)
+        for t in range(PACK):
+            den = bank("B", t, "den%d" % t)
+            for jb in range(4):
+                turned_sum(den[:, block(jb)], brows[t][:, block(jb)], g9[t][:, block(jb)])
+            root = new([P, S], F32, "root%d" % t)
+            nc.scalar.activation(root[:], den[:], ACT.Abs_reciprocal_sqrt, bias=eight[:])
+            back = bank("B", t, "back%d" % t)
+            for jb in range(4):
+                nc.tensor.transpose(back[:, block(jb)], root[:, block(jb)], ident[:])
+            a = rows[t]
+            if t == 0:
+                nc.vector.tensor_copy(a[:, :S], accs[t][:])
+            else:
+                nc.scalar.activation(a[:, :S], accs[t][:], ACT.Copy)
+            inv = new([P, S], F32, "inv%d" % t)
+            nc.scalar.activation(inv[:], back[:], ACT.Square)
+            g8 = new([P, S], F32, "g8_%d" % t)
+            gather("scalar" if t == 3 else "vector", g8[:], a[:], l_n8[:])
+            num = new([P, S], F32, "num%d" % t)
+            nc.vector.tensor_tensor(num[:], a[:, :S], g8[:], ALU.subtract)
+            res = new([P, S], F32, "res%d" % t)
+            nc.vector.tensor_tensor(res[:], num[:], inv[:], ALU.mult)
+            nc.sync.dma_start(out_rows[t], res[:])

@@ -28,6 +28,7 @@ def tile_picked_cdkeynormbdettrim_none_p_kernel(tc, x_words, x_scales, w1, gs, g
         lists = ctx.enter_context(tc.tile_pool(name="lists", bufs=1))
         sb = ctx.enter_context(tc.tile_pool(name="sb", bufs=1))
         head = ctx.enter_context(tc.tile_pool(name="head", bufs=1))
+        ring = ctx.enter_context(tc.tile_pool(name="ring", bufs=1))
         psum = ctx.enter_context(tc.psum_pool(name="psum", bufs=1))
 
         def new(shape, dtype, name, tag=None):
@@ -35,6 +36,9 @@ def tile_picked_cdkeynormbdettrim_none_p_kernel(tc, x_words, x_scales, w1, gs, g
 
         def after_w(shape, dtype, name, offset):
             return head.tile(shape, dtype, name=name, align_bytes=64, offset=offset)
+
+        def in_ring(shape, name, offset, dtype=F32):
+            return ring.tile(shape, dtype, name=name, align_bytes=64, offset=offset)
 
         def load_list(src, name):
             tile = lists.tile([P, LCOLS], U16, name=name)
@@ -46,12 +50,14 @@ def tile_picked_cdkeynormbdettrim_none_p_kernel(tc, x_words, x_scales, w1, gs, g
 
         xs = new([P, T], U8, "xs")
         nc.gpsimd.memset(xs[:].bitcast(I32), 0)
+        eight = new([P, 1], F32, "eight")
+        nc.gpsimd.memset(eight[:], 8.0)
         ds = new([P, G], U8, "ds")
         nc.gpsimd.memset(ds[:].bitcast(I32), 0)
         key_scales = new([P, S], U8, "key_scales")
         nc.gpsimd.memset(key_scales[:].bitcast(I32), 0)
-        eight = new([P, 1], F32, "eight")
-        nc.gpsimd.memset(eight[:], 8.0)
+        warm = new([P, 1], F32, "warm")
+        nc.scalar.activation(warm[:], eight[:], ACT.Abs_reciprocal_sqrt, bias=eight[:])
         ident = new([P, P], F32, "ident")
         make_identity(nc, ident[:])
         rows = [new([P, 2 * S], F32, "rows%d" % t) for t in range(PACK)]
@@ -62,23 +68,22 @@ def tile_picked_cdkeynormbdettrim_none_p_kernel(tc, x_words, x_scales, w1, gs, g
         xs_rows = x_scales[0].bitcast(I32)
         for r in range(4):
             nc.sync.dma_start(xs[r:P:32, :].bitcast(I32), xs_rows[r:16:4, :])
+        l_cand = load_list(cand, "l_cand")
+        l_n7 = load_list(n7, "l_n7")
+        l_n5 = load_list(n5, "l_n5")
         xw = new([P, T], U32, "xw")
         nc.sync.dma_start(xw[:].bitcast(I32), x_words[0].rearrange("p n t -> p (n t)").bitcast(I32))
         w_rows = w1.rearrange("(p j) c -> p j c", j=PACK)
         w_raw = []
         for h in range(2):
-            wr = new([P, PACK, HALF], F32, "w_raw%d" % h)
+            wr = in_ring([P, PACK, HALF], "w_raw%d" % h, 4096 * h)
             nc.sync.dma_start(wr[:], w_rows[:, :, h * HALF:(h + 1) * HALF])
             w_raw.append(wr)
         l_n6 = load_list(n6, "l_n6")
-        l_n7 = load_list(n7, "l_n7")
-        l_cand = load_list(cand, "l_cand")
-        l_n5 = load_list(n5, "l_n5")
         dw = new([P, G], U32, "dw")
         nc.sync.dma_start(dw[:].bitcast(I32), d_words[0].rearrange("p n t -> p (n t)").bitcast(I32))
         l_k1 = load_list(k1, "l_k1")
-        ds_rows = d_scales[0].bitcast(I32)
-        nc.sync.dma_start(ds[0:P:8, :].bitcast(I32), ds_rows)
+        nc.sync.dma_start(ds[0:P:8, :].bitcast(I32), d_scales[0].bitcast(I32))
         l_n1 = load_list(n1, "l_n1")
         l_n2 = load_list(n2, "l_n2")
         l_n3 = load_list(n3, "l_n3")
@@ -91,6 +96,9 @@ def tile_picked_cdkeynormbdettrim_none_p_kernel(tc, x_words, x_scales, w1, gs, g
         tok_words = new([P, S], U32, "tok_words")
         nc.vector.tensor_copy(tok_words[:], xw[:].indirect(l_offs[:]))
 
+        cand_words_l = new([P, S], U32, "cand_words_l")
+        nc.vector.tensor_copy(cand_words_l[:], xw[:].indirect(l_cand[:]))
+
         w_bf = after_w([P, PACK, P, PACK], BF16, "w_bf", 0)
         for q in range(4):
             src = w_raw[q // 2][:, :, (q % 2) * P:(q % 2 + 1) * P].rearrange("p j (m t) -> p m j t", t=PACK)
@@ -99,9 +107,9 @@ def tile_picked_cdkeynormbdettrim_none_p_kernel(tc, x_words, x_scales, w1, gs, g
                 nc.scalar.copy(dst, src)
             else:
                 nc.vector.tensor_copy(dst, src)
-        gk_b = new([P, K], F32, "gk_b", "w_raw0")
+        gk_b = in_ring([P, K], "gk_b", 1024)
         nc.sync.dma_start(gk_b[:], gk.rearrange("k o -> (k o)").partition_broadcast(P))
-        gs_b = new([P, K], F32, "gs_b", "w_raw1")
+        gs_b = in_ring([P, K], "gs_b", 4096)
         nc.sync.dma_start(gs_b[:], gs.rearrange("k o -> (k o)").partition_broadcast(P))
         w_codes = new([P, S], U32, "w_codes")
         w_scales = new([P, S], U8, "w_scales")
@@ -109,9 +117,9 @@ def tile_picked_cdkeynormbdettrim_none_p_kernel(tc, x_words, x_scales, w1, gs, g
             cols = slice(t * P, (t + 1) * P)
             nc.vector.quantize_mx(out=w_codes[:, cols].bitcast(FP8X4), scales=w_scales[:, cols], in_=w_bf[:, t].rearrange("p m j -> p (m j)"))
 
-        def product(acc, t, lw, ls, rw, rs):
+        def product(acc, t, lw, ls, rw, rs, places=slice(0, S)):
             cols = slice(t * P, (t + 1) * P)
-            nc.tensor.matmul_mx(out=acc[:], lhsT=lw[:, cols].bitcast(FP8X4), lhsT_scale=ls[:, cols], rhs=rw[:].bitcast(FP8X4), rhs_scale=rs[:], start=True, stop=True)
+            nc.tensor.matmul_mx(out=acc[:, places], lhsT=lw[:, cols].bitcast(FP8X4), lhsT_scale=ls[:, cols], rhs=rw[:, places].bitcast(FP8X4), rhs_scale=rs[:, places], start=True, stop=True)
 
         def deal_words(dst, src):
             nc.vector.tensor_copy(dst[:].rearrange("p (t c i) -> p c t i", t=PACK, i=4), src[:].rearrange("p (c i t) -> p c t i", t=PACK, i=4))
@@ -135,8 +143,12 @@ def tile_picked_cdkeynormbdettrim_none_p_kernel(tc, x_words, x_scales, w1, gs, g
         def block(n):
             return slice(n * P, (n + 1) * P)
 
+        def add_turned(banks, t, term, start=False, stop=False):
+            for jb in range(4):
+                nc.tensor.matmul(banks[jb][:, block(t)], term[:, block(jb)], ident[:], start=start, stop=stop, is_transpose=True)
+
         def quantise(name, turned, gain):
-            woven = new([P, S, PACK], BF16, name + "_bf")
+            woven = in_ring([P, S, PACK], name + "_bf", 8192, BF16)
             codes = new([P, S], U32, name + "_codes")
             scales = new([P, S], U8, name + "_scales")
             gain_v = gain[:].rearrange("j (p t) -> j p t", t=PACK)
@@ -162,14 +174,8 @@ def tile_picked_cdkeynormbdettrim_none_p_kernel(tc, x_words, x_scales, w1, gs, g
             ys.append(bank("A", t, "y%d" % t))
             product(ys[t], t, w_codes, w_scales, tok_words, tok_scales)
 
-        cand_words_l = after_w([P, S], U32, "cand_words_l", 0)
-        nc.vector.tensor_copy(cand_words_l[:], xw[:].indirect(l_cand[:]))
         cand_scales_l = after_w([P, S], U8, "cand_scales_l", 2048)
         nc.vector.tensor_copy(cand_scales_l[:], xs[:].indirect(l_cand[:]))
-        cand_words = new([P, S], U32, "cand_words")
-        deal_words(cand_words, cand_words_l)
-        cand_scales = new([P, S], U8, "cand_scales")
-        deal_bytes(cand_scales, cand_scales_l)
         key_scales_l = after_w([P, S], U8, "key_scales_l", 2560)
         nc.vector.tensor_copy(key_scales_l[:], ds[:].indirect(l_k1[:]))
         key_words_l = after_w([P, S], U32, "key_words_l", 3072)
@@ -183,70 +189,86 @@ def tile_picked_cdkeynormbdettrim_none_p_kernel(tc, x_words, x_scales, w1, gs, g
             nc.sync.dma_start(key_scales[e:P:32, :].bitcast(I32), key_scales_d[first:P:32, :].bitcast(I32))
 
         turned = [bank("B", jb, "z2_turned%d" % jb) for jb in range(4)]
+        cuts = []
         brows = [new([P, 2 * S], F32, "brows%d" % t) for t in range(PACK)]
         for t in range(PACK):
             y = rows[t]
             nc.scalar.activation(y[:, :S], ys[t][:], ACT.Copy)
-            g6 = brows[t][:, S:]
-            g7 = new([P, S], F32, "g7_%d" % t)
-            gather("scalar", g6, y[:], l_n6[:])
-            gather("scalar", g7[:], y[:], l_n7[:])
-            m = new([P, S], F32, "m_%d" % t)
-            nc.vector.tensor_tensor(m[:], g6, g7[:], ALU.max)
-            u = new([P, S], F32, "u_%d" % t)
-            nc.vector.tensor_tensor(u[:], y[:].indirect(l_n5[:]), m[:], ALU.subtract)
-            for jb in range(4):
-                turned_sum(turned[jb][:, block(t)], y[:, block(jb)], u[:, block(jb)])
+            g7 = brows[t][:, S:]
+            gather("scalar", g7, y[:], l_n7[:], -1.0)
+            lead = new([P, S], F32, "lead%d" % t)
+            nc.vector.tensor_tensor(lead[:], y[:].indirect(l_n6[:]), g7, ALU.add)
+            g5 = new([P, S], F32, "g5_%d" % t)
+            gather("vector" if t == 2 else "scalar", g5[:], y[:], l_n5[:])
+            cut = new([P, S], F32, "cut%d" % t)
+            nc.vector.tensor_scalar(cut[:], lead[:], -1.0, 0.0, ALU.mult, ALU.min)
+            cuts.append(cut)
+            for n, term in enumerate((y[:, :S], g7, g5[:])):
+                add_turned(turned, t, term, start=(t == 0 and n == 0))
+            if t % 2 == 1:
+                for s in (t - 1, t):
+                    add_turned(turned, s, cuts[s][:], stop=(s == PACK - 1))
+        cand_words = new([P, S], U32, "cand_words", "lead3")
+        deal_words(cand_words, cand_words_l)
+        cand_scales = new([P, S], U8, "cand_scales", "lead2")
+        deal_bytes(cand_scales, cand_scales_l)
         z2_codes, z2_scales = quantise("z2", turned, gk_b)
+
+        turned = [bank("B", jb, "z_turned%d" % jb) for jb in range(4)]
+        for t in range(PACK):
+            y = rows[t]
+            for n, (la, lb, factor, nm) in enumerate(((l_n1, l_n2, 0.75, "12"), (l_n3, l_n4, -0.75, "34"))):
+                g = new([P, S], F32, "g%s_%d" % (nm, t), ("g0", "g1", "g2", "z2_flat3")[(2 * t + n) % 4])
+                gather("scalar", g[:], y[:], la[:], factor)
+                pr = in_ring([P, S], "p%s_%d" % (nm, t), 2048 * n)
+                nc.vector.tensor_tensor(pr[:], y[:].indirect(lb[:]), g[:], ALU.mult)
+                for jb in range(4):
+                    nc.tensor.matmul(turned[jb][:, block(t)], pr[:, block(jb)], ident[:], start=(n == 0), stop=(n == 1), is_transpose=True)
 
         for t in range(PACK):
             acc = bank("A", (t + 2) % 4, "b%d" % t)
             product(acc, t, key_words, key_scales, z2_codes, z2_scales)
             nc.scalar.activation(brows[t][:, :S], acc[:], ACT.Abs)
-
-        turned = [bank("B", jb, "z_turned%d" % jb) for jb in range(4)]
-        for t in range(PACK):
-            y = rows[t]
-            prods = []
-            for (la, lb, factor, nm) in ((l_n1, l_n2, 0.75, "12"), (l_n3, l_n4, -0.75, "34")):
-                g = new([P, S], F32, "g%s_%d" % (nm, t))
-                gather("scalar", g[:], y[:], la[:], factor)
-                pr = new([P, S], F32, "p%s_%d" % (nm, t), "z2_bf" if (nm, t) == ("12", 2) else None)
-                nc.vector.tensor_tensor(pr[:], y[:].indirect(lb[:]), g[:], ALU.mult)
-                prods.append(pr)
-            for jb in range(4):
-                turned_sum(turned[jb][:, block(t)], prods[0][:, block(jb)], prods[1][:, block(jb)])
-        g9 = []
-        for t in range(PACK):
-            g9.append(new([P, S], F32, "g9_%d" % t))
+        g9 = [new([P, S], F32, "g9_%d" % t) for t in range(3)]
+        for t in range(3):
             gather("scalar", g9[t][:], brows[t][:], l_n9[:])
         z_codes, z_scales = quantise("z", turned, gs_b)
+        g9.append(in_ring([P, S], "g9_3", 4096))
+        gather("vector", g9[3][:], brows[3][:], l_n9[:])
 
-        out_rows = out.rearrange("(p t) n -> t p n", t=PACK)
-        accs = []
-        for t in range(PACK):
-            accs.append(bank("A", (t + 2) % 4, "a%d" % t))
-            product(accs[t], t, cand_words, cand_scales, z_codes, z_scales)
-        for t in range(PACK):
+
+        def inverse(t):
             den = bank("B", t, "den%d" % t)
             for jb in range(4):
                 turned_sum(den[:, block(jb)], brows[t][:, block(jb)], g9[t][:, block(jb)])
             root = new([P, S], F32, "root%d" % t)
             nc.scalar.activation(root[:], den[:], ACT.Abs_reciprocal_sqrt, bias=eight[:])
-            back = bank("B", t, "back%d" % t)
+            inv_t = in_ring([P, S], "inv_t%d" % t, 8192 + 2048 * (t % 2))
+            nc.gpsimd.tensor_tensor(inv_t[:], root[:], root[:], ALU.mult)
+            return inv_t
+
+        out_rows = out.rearrange("(p t) n -> t p n", t=PACK)
+        inv_t = [inverse(t) for t in range(PACK - 1)]
+        accs = [bank("A", (t + 2) % 4, "a%d" % t) for t in range(PACK)]
+        for t in range(PACK):
+            product(accs[t], t, cand_words, cand_scales, z_codes, z_scales)
+        nc.vector.tensor_copy(rows[0][:, :S], accs[0][:])
+        inv_t.append(inverse(PACK - 1))
+        for t in range(PACK):
+            inv = bank("B", t, "inv%d" % t)
             for jb in range(4):
-                nc.tensor.transpose(back[:, block(jb)], root[:, block(jb)], ident[:])
-            a = rows[t]
-            if t == 0:
-                nc.vector.tensor_copy(a[:, :S], accs[t][:])
-            else:
-                nc.scalar.activation(a[:, :S], accs[t][:], ACT.Copy)
-            inv = new([P, S], F32, "inv%d" % t)
-            nc.scalar.activation(inv[:], back[:], ACT.Square)
+                nc.tensor.transpose(inv[:, block(jb)], inv_t[t][:, block(jb)], ident[:])
+            if t > 0:
+                nc.scalar.activation(rows[t][:, :S], accs[t][:], ACT.Copy)
             g8 = new([P, S], F32, "g8_%d" % t)
-            gather("scalar" if t == 3 else "vector", g8[:], a[:], l_n8[:])
             num = new([P, S], F32, "num%d" % t)
-            nc.vector.tensor_tensor(num[:], a[:, :S], g8[:], ALU.subtract)
             res = new([P, S], F32, "res%d" % t)
-            nc.vector.tensor_tensor(res[:], num[:], inv[:], ALU.mult)
-            nc.sync.dma_start(out_rows[t], res[:])
+            if t == 1:
+                for engine, (cols, lc) in zip(("vector", "scalar"), halves()):
+                    gather(engine, g8[:, cols], rows[t][:], l_n8[:, lc])
+            for cols, lc in (halves() if t == PACK - 1 else [(slice(0, S), slice(0, LCOLS))]):
+                if t != 1:
+                    gather("scalar" if t > 0 else "vector", g8[:, cols], rows[t][:], l_n8[:, lc])
+                nc.vector.tensor_tensor(num[:, cols], accs[t][:, cols], g8[:, cols], ALU.subtract)
+                nc.vector.tensor_tensor(res[:, cols], inv[:, cols], num[:, cols], ALU.mult)
+                nc.sync.dma_start(out_rows[t][:, cols], res[:, cols])

@@ -68,17 +68,17 @@ def tile_picked_cdkeynormbdettrim_none_p_kernel(tc, x_words, x_scales, w1, gs, g
         xs_rows = x_scales[0].bitcast(I32)
         for r in range(4):
             nc.sync.dma_start(xs[r:P:32, :].bitcast(I32), xs_rows[r:16:4, :])
-        l_cand = load_list(cand, "l_cand")
-        l_n7 = load_list(n7, "l_n7")
-        l_n5 = load_list(n5, "l_n5")
         xw = new([P, T], U32, "xw")
         nc.sync.dma_start(xw[:].bitcast(I32), x_words[0].rearrange("p n t -> p (n t)").bitcast(I32))
+        l_cand = load_list(cand, "l_cand")
         w_rows = w1.rearrange("(p j) c -> p j c", j=PACK)
         w_raw = []
         for h in range(2):
             wr = in_ring([P, PACK, HALF], "w_raw%d" % h, 4096 * h)
             nc.sync.dma_start(wr[:], w_rows[:, :, h * HALF:(h + 1) * HALF])
             w_raw.append(wr)
+        l_n7 = load_list(n7, "l_n7")
+        l_n5 = load_list(n5, "l_n5")
         l_n6 = load_list(n6, "l_n6")
         dw = new([P, G], U32, "dw")
         nc.sync.dma_start(dw[:].bitcast(I32), d_words[0].rearrange("p n t -> p (n t)").bitcast(I32))
@@ -151,16 +151,16 @@ def tile_picked_cdkeynormbdettrim_none_p_kernel(tc, x_words, x_scales, w1, gs, g
             woven = in_ring([P, S, PACK], name + "_bf", 8192, BF16)
             codes = new([P, S], U32, name + "_codes")
             scales = new([P, S], U8, name + "_scales")
-            gain_v = gain[:].rearrange("j (p t) -> j p t", t=PACK)
+            gain_v = gain[:].rearrange("j (p u e) -> j u p e", u=2, e=2)
             for h in range(2):
                 pairs = bank("A", h, name + "_pairs%d" % h)
                 for b2 in range(2):
                     jb = 2 * h + b2
-                    flat = new([P, K], BF16, name + "_flat%d" % jb)
-                    nc.vector.tensor_tensor(flat[:].rearrange("j (p t) -> j p t", t=PACK), turned[jb][:].rearrange("j (t p) -> j p t", t=PACK), gain_v, ALU.mult)
+                    flat = in_ring([P, K], name + "_flat3", 13824, BF16) if jb == 3 else new([P, K], BF16, name + "_flat%d" % jb)
+                    nc.vector.tensor_tensor(flat[:].rearrange("j (u p e) -> j u p e", u=2, e=2), turned[jb][:].rearrange("j (u e p) -> j u p e", u=2, e=2), gain_v, ALU.mult)
                     words = flat[:].bitcast(F32)
                     for u in range(2):
-                        nc.tensor.transpose(pairs[:, block(2 * b2 + u)], words[:, u:2 * P:2], ident[:])
+                        nc.tensor.transpose(pairs[:, block(2 * b2 + u)], words[:, block(u)], ident[:])
                 cols = slice(h * HALF, (h + 1) * HALF)
                 dst = woven[:, cols, :].rearrange("p c t -> p (c t)")
                 nc.scalar.copy(dst.bitcast(F32).rearrange("p (b j u) -> p b j u", b=2, u=2), pairs[:].rearrange("p (b u j) -> p b j u", b=2, u=2))
@@ -189,86 +189,101 @@ def tile_picked_cdkeynormbdettrim_none_p_kernel(tc, x_words, x_scales, w1, gs, g
             nc.sync.dma_start(key_scales[e:P:32, :].bitcast(I32), key_scales_d[first:P:32, :].bitcast(I32))
 
         turned = [bank("B", jb, "z2_turned%d" % jb) for jb in range(4)]
-        cuts = []
         brows = [new([P, 2 * S], F32, "brows%d" % t) for t in range(PACK)]
-        for t in range(PACK):
-            y = rows[t]
-            nc.scalar.activation(y[:, :S], ys[t][:], ACT.Copy)
-            g7 = brows[t][:, S:]
-            gather("scalar", g7, y[:], l_n7[:], -1.0)
-            lead = new([P, S], F32, "lead%d" % t)
-            nc.vector.tensor_tensor(lead[:], y[:].indirect(l_n6[:]), g7, ALU.add)
-            g5 = new([P, S], F32, "g5_%d" % t)
-            gather("vector" if t == 2 else "scalar", g5[:], y[:], l_n5[:])
-            cut = new([P, S], F32, "cut%d" % t)
-            nc.vector.tensor_scalar(cut[:], lead[:], -1.0, 0.0, ALU.mult, ALU.min)
-            cuts.append(cut)
-            for n, term in enumerate((y[:, :S], g7, g5[:])):
-                add_turned(turned, t, term, start=(t == 0 and n == 0))
-            if t % 2 == 1:
-                for s in (t - 1, t):
-                    add_turned(turned, s, cuts[s][:], stop=(s == PACK - 1))
+        g7 = [brows[t][:, S:] for t in range(PACK)]
+        g5 = [new([P, S], F32, "g5_%d" % t) for t in range(PACK)]
+        cut = [new([P, S], F32, "cut%d" % t) for t in range(PACK)]
+        for pair in ((0, 1), (2, 3)):
+            for t in pair:
+                nc.scalar.activation(rows[t][:, :S], ys[t][:], ACT.Copy)
+            for t in pair:
+                gather("scalar", g7[t], rows[t][:], l_n7[:], -1.0)
+        for t in (0, 1, 3):
+            gather("scalar", g5[t][:], rows[t][:], l_n5[:])
+        for pair in ((0, 1), (2, 3)):
+            lead = {t: new([P, S], F32, "lead%d" % t) for t in pair}
+            for t in pair:
+                nc.vector.tensor_tensor(lead[t][:], rows[t][:].indirect(l_n6[:]), g7[t], ALU.add)
+            for t in pair:
+                nc.vector.tensor_scalar(cut[t][:], lead[t][:], -1.0, 0.0, ALU.mult, ALU.min)
+            if pair[0] == 0:
+                nc.vector.tensor_tensor(g5[2][:], rows[2][:].indirect(l_n5[:]), g7[2], ALU.add)
+        terms = [(t, rows[t][:, :S]) for t in range(PACK)] + [(t, g7[t]) for t in (0, 1, 3)]
+        terms += [(0, cut[0][:]), (1, cut[1][:])] + [(t, g5[t][:]) for t in (2, 0, 1)]
+        for n, (t, term) in enumerate(terms):
+            add_turned(turned, t, term, start=(n == 0))
+        for jb in range(4):
+            for t, term in ((3, g5[3]), (2, cut[2]), (3, cut[3])):
+                nc.tensor.matmul(turned[jb][:, block(t)], term[:, block(jb)], ident[:], start=False, stop=(term is cut[3]), is_transpose=True)
         cand_words = new([P, S], U32, "cand_words", "lead3")
         deal_words(cand_words, cand_words_l)
         cand_scales = new([P, S], U8, "cand_scales", "lead2")
         deal_bytes(cand_scales, cand_scales_l)
         z2_codes, z2_scales = quantise("z2", turned, gk_b)
 
+        b_acc = [bank("A", (t + 2) % 4, "b%d" % t) for t in range(PACK)]
+        for t in range(PACK):
+            product(b_acc[t], t, key_words, key_scales, z2_codes, z2_scales)
         turned = [bank("B", jb, "z_turned%d" % jb) for jb in range(4)]
         for t in range(PACK):
             y = rows[t]
             for n, (la, lb, factor, nm) in enumerate(((l_n1, l_n2, 0.75, "12"), (l_n3, l_n4, -0.75, "34"))):
-                g = new([P, S], F32, "g%s_%d" % (nm, t), ("g0", "g1", "g2", "z2_flat3")[(2 * t + n) % 4])
+                slot = ("g12_0", 16384, "z2_flat1", 14336, 16384, "z2_flat1", 14336, 16384)[2 * t + n]
+                g = new([P, S], F32, "g%s_%d" % (nm, t), slot) if isinstance(slot, str) else in_ring([P, S], "g%s_%d" % (nm, t), slot)
                 gather("scalar", g[:], y[:], la[:], factor)
-                pr = in_ring([P, S], "p%s_%d" % (nm, t), 2048 * n)
-                nc.vector.tensor_tensor(pr[:], y[:].indirect(lb[:]), g[:], ALU.mult)
+                pr = in_ring([P, S], "p%s_%d" % (nm, t), 2048 * n) if t % 2 == 1 else new([P, S], F32, "p%s_%d" % (nm, t), ("g5_3", "z2_flat2")[n])
+                if (t, n) == (0, 0):
+                    other = new([P, S], F32, "other")
+                    gather("scalar", other[:], y[:], lb[:])
+                    nc.gpsimd.tensor_tensor(pr[:], g[:], other[:], ALU.mult)
+                else:
+                    nc.vector.tensor_tensor(pr[:], y[:].indirect(lb[:]), g[:], ALU.mult)
                 for jb in range(4):
                     nc.tensor.matmul(turned[jb][:, block(t)], pr[:, block(jb)], ident[:], start=(n == 0), stop=(n == 1), is_transpose=True)
 
-        for t in range(PACK):
-            acc = bank("A", (t + 2) % 4, "b%d" % t)
-            product(acc, t, key_words, key_scales, z2_codes, z2_scales)
-            nc.scalar.activation(brows[t][:, :S], acc[:], ACT.Abs)
-        g9 = [new([P, S], F32, "g9_%d" % t) for t in range(3)]
-        for t in range(3):
-            gather("scalar", g9[t][:], brows[t][:], l_n9[:])
+        twin, den = {}, {}
+        for t in (2, 0, 1, 3):
+            nc.scalar.activation(brows[t][:, :S], b_acc[t][:], ACT.Abs)
+            if t >= 2:
+                twin[t] = new([P, S], F32, "twin%d" % t)
+                nc.sync.dma_start(twin[t][:], brows[t][:, :S])
+            else:
+                g9 = new([P, S], F32, "g9_%d" % t)
+                gather("scalar", g9[:], brows[t][:], l_n9[:])
+                den[t] = in_ring([P, S], "den0", 16384) if t == 0 else new([P, S], F32, "den1")
+                nc.gpsimd.tensor_tensor(den[t][:], brows[t][:, :S], g9[:], ALU.add)
         z_codes, z_scales = quantise("z", turned, gs_b)
-        g9.append(in_ring([P, S], "g9_3", 4096))
-        gather("vector", g9[3][:], brows[3][:], l_n9[:])
-
+        for t, offset in ((2, 4096), (3, 8192)):
+            den[t] = in_ring([P, S], "den%d" % t, offset)
+            nc.vector.tensor_tensor(den[t][:], brows[t][:].indirect(l_n9[:]), twin[t][:], ALU.add)
 
         def inverse(t):
-            den = bank("B", t, "den%d" % t)
-            for jb in range(4):
-                turned_sum(den[:, block(jb)], brows[t][:, block(jb)], g9[t][:, block(jb)])
-            root = new([P, S], F32, "root%d" % t)
-            nc.scalar.activation(root[:], den[:], ACT.Abs_reciprocal_sqrt, bias=eight[:])
-            inv_t = in_ring([P, S], "inv_t%d" % t, 8192 + 2048 * (t % 2))
-            nc.gpsimd.tensor_tensor(inv_t[:], root[:], root[:], ALU.mult)
+            root = new([P, S], F32, "root%d" % t) if t != 2 else in_ring([P, S], "root2", 12288)
+            nc.scalar.activation(root[:], den[t][:], ACT.Abs_reciprocal_sqrt, bias=eight[:])
+            if t < 2:
+                inv_t = new([P, S], F32, "inv_t%d" % t)
+                nc.scalar.activation(inv_t[:], root[:], ACT.Square)
+            else:
+                inv_t = new([P, S], F32, "inv_t2", "twin3") if t == 2 else in_ring([P, S], "inv_t3", 12288)
+                nc.gpsimd.tensor_tensor(inv_t[:], root[:], root[:], ALU.mult)
             return inv_t
 
         out_rows = out.rearrange("(p t) n -> t p n", t=PACK)
         inv_t = [inverse(t) for t in range(PACK - 1)]
-        accs = [bank("A", (t + 2) % 4, "a%d" % t) for t in range(PACK)]
+        accs = [bank("B", t, "a%d" % t) for t in range(PACK)]
         for t in range(PACK):
             product(accs[t], t, cand_words, cand_scales, z_codes, z_scales)
-        nc.vector.tensor_copy(rows[0][:, :S], accs[0][:])
+        nc.scalar.activation(rows[0][:, :S], accs[0][:], ACT.Copy)
+        nc.vector.tensor_copy(rows[1][:, :S], accs[1][:])
         inv_t.append(inverse(PACK - 1))
         for t in range(PACK):
-            inv = bank("B", t, "inv%d" % t)
-            for jb in range(4):
-                nc.tensor.transpose(inv[:, block(jb)], inv_t[t][:, block(jb)], ident[:])
-            if t > 0:
+            if t > 1:
                 nc.scalar.activation(rows[t][:, :S], accs[t][:], ACT.Copy)
             g8 = new([P, S], F32, "g8_%d" % t)
             num = new([P, S], F32, "num%d" % t)
             res = new([P, S], F32, "res%d" % t)
-            if t == 1:
-                for engine, (cols, lc) in zip(("vector", "scalar"), halves()):
-                    gather(engine, g8[:, cols], rows[t][:], l_n8[:, lc])
             for cols, lc in (halves() if t == PACK - 1 else [(slice(0, S), slice(0, LCOLS))]):
-                if t != 1:
-                    gather("scalar" if t > 0 else "vector", g8[:, cols], rows[t][:], l_n8[:, lc])
+                gather("scalar" if t > 0 else "vector", g8[:, cols], rows[t][:], l_n8[:, lc])
                 nc.vector.tensor_tensor(num[:, cols], accs[t][:, cols], g8[:, cols], ALU.subtract)
-                nc.vector.tensor_tensor(res[:, cols], inv[:, cols], num[:, cols], ALU.mult)
+                nc.vector.tensor_tensor(res[:, cols], inv_t[t][:, cols], num[:, cols], ALU.mult)
                 nc.sync.dma_start(out_rows[t][:, cols], res[:, cols])

@@ -18,8 +18,26 @@ ACT = mybir.ActivationFunctionType
 
 P = 128
 PACK = 4
+BLOCKS = S // P
 HALF = S // 2
-LCOLS = S // 16
+LIST_COLS = S // 16
+TILE_BYTES = 4 * S
+
+W_RAW_AT = (0, 2 * TILE_BYTES)
+GK_ROW_AT = TILE_BYTES // 2
+GS_ROW_AT = 2 * TILE_BYTES
+PRODUCT_AT = (0, TILE_BYTES)
+SUM_AT = (GS_ROW_AT - TILE_BYTES // 2, GS_ROW_AT + TILE_BYTES // 2)
+WOVEN_AT = 4 * TILE_BYTES
+BEFORE_FLAT_AT = 6 * TILE_BYTES
+LAST_FLAT_AT = 7 * TILE_BYTES - TILE_BYTES // 4
+AFTER_FLAT_AT = 7 * TILE_BYTES
+CHAIN_AT = 8 * TILE_BYTES
+
+CAND_SCALES_AT, KEY_SCALES_AT, KEY_WORDS_AT = TILE_BYTES, TILE_BYTES + S, TILE_BYTES + 2 * S
+
+VECTOR_N5_TILE = 2
+FUSED_SUM_TILES = (2, 3)
 
 
 def tile_picked_cdkeynormbdettrim_none_p_kernel(tc, x_words, x_scales, w1, gs, gk, d_words, d_scales, offs, n1, n2, n3, n4, n5, n6, n7, cand, k1, n8, n9, out):
@@ -31,29 +49,35 @@ def tile_picked_cdkeynormbdettrim_none_p_kernel(tc, x_words, x_scales, w1, gs, g
         ring = ctx.enter_context(tc.tile_pool(name="ring", bufs=1))
         psum = ctx.enter_context(tc.psum_pool(name="psum", bufs=1))
 
-        def new(shape, dtype, name, tag=None):
-            return sb.tile(shape, dtype, name=name, tag=tag or name, align_bytes=64)
+        def new(shape, dtype, name, after=None):
+            return sb.tile(shape, dtype, name=name, tag=after or name, align_bytes=64)
 
-        def after_w(shape, dtype, name, offset):
+        def in_head(shape, dtype, name, offset):
             return head.tile(shape, dtype, name=name, align_bytes=64, offset=offset)
 
         def in_ring(shape, name, offset, dtype=F32):
             return ring.tile(shape, dtype, name=name, align_bytes=64, offset=offset)
 
+        def bank(kind, n, name):
+            return psum.tile([P, S], F32, name=name, tag="%s%d" % (kind, n))
+
+        def block(n):
+            return slice(n * P, (n + 1) * P)
+
         def load_list(src, name):
-            tile = lists.tile([P, LCOLS], U16, name=name)
+            tile = lists.tile([P, LIST_COLS], U16, name=name)
             nc.sync.dma_start(tile[:], src)
             return tile
 
-        def halves():
-            return [(slice(h * HALF, (h + 1) * HALF), slice(h * LCOLS // 2, (h + 1) * LCOLS // 2)) for h in range(2)]
+        def scalar_gather(dst, window, offsets, scale=1.0):
+            nc.scalar.activation(dst, window.indirect(offsets), ACT.Copy, scale=scale)
 
-        xs = new([P, T], U8, "xs")
-        nc.gpsimd.memset(xs[:].bitcast(I32), 0)
+        x_bytes = new([P, T], U8, "x_bytes")
+        nc.gpsimd.memset(x_bytes[:].bitcast(I32), 0)
         eight = new([P, 1], F32, "eight")
         nc.gpsimd.memset(eight[:], 8.0)
-        ds = new([P, G], U8, "ds")
-        nc.gpsimd.memset(ds[:].bitcast(I32), 0)
+        d_bytes = new([P, G], U8, "d_bytes")
+        nc.gpsimd.memset(d_bytes[:].bitcast(I32), 0)
         key_scales = new([P, S], U8, "key_scales")
         nc.gpsimd.memset(key_scales[:].bitcast(I32), 0)
         warm = new([P, 1], F32, "warm")
@@ -65,25 +89,24 @@ def tile_picked_cdkeynormbdettrim_none_p_kernel(tc, x_words, x_scales, w1, gs, g
             nc.vector.memset(rows[t][:, S:], 0.0)
 
         l_offs = load_list(offs, "l_offs")
-        xs_rows = x_scales[0].bitcast(I32)
+        x_scale_rows = x_scales[0].bitcast(I32)
         for r in range(4):
-            nc.sync.dma_start(xs[r:P:32, :].bitcast(I32), xs_rows[r:16:4, :])
-        xw = new([P, T], U32, "xw")
-        nc.sync.dma_start(xw[:].bitcast(I32), x_words[0].rearrange("p n t -> p (n t)").bitcast(I32))
+            nc.sync.dma_start(x_bytes[r:P:32, :].bitcast(I32), x_scale_rows[r:16:4, :])
+        x_table = new([P, T], U32, "x_table")
+        nc.sync.dma_start(x_table[:].bitcast(I32), x_words[0].rearrange("p n t -> p (n t)").bitcast(I32))
         l_cand = load_list(cand, "l_cand")
         w_rows = w1.rearrange("(p j) c -> p j c", j=PACK)
         w_raw = []
         for h in range(2):
-            wr = in_ring([P, PACK, HALF], "w_raw%d" % h, 4096 * h)
-            nc.sync.dma_start(wr[:], w_rows[:, :, h * HALF:(h + 1) * HALF])
-            w_raw.append(wr)
+            w_raw.append(in_ring([P, PACK, HALF], "w_raw%d" % h, W_RAW_AT[h]))
+            nc.sync.dma_start(w_raw[h][:], w_rows[:, :, h * HALF:(h + 1) * HALF])
         l_n7 = load_list(n7, "l_n7")
         l_n5 = load_list(n5, "l_n5")
         l_n6 = load_list(n6, "l_n6")
-        dw = new([P, G], U32, "dw")
-        nc.sync.dma_start(dw[:].bitcast(I32), d_words[0].rearrange("p n t -> p (n t)").bitcast(I32))
+        d_table = new([P, G], U32, "d_table")
+        nc.sync.dma_start(d_table[:].bitcast(I32), d_words[0].rearrange("p n t -> p (n t)").bitcast(I32))
         l_k1 = load_list(k1, "l_k1")
-        nc.sync.dma_start(ds[0:P:8, :].bitcast(I32), d_scales[0].bitcast(I32))
+        nc.sync.dma_start(d_bytes[0:P:8, :].bitcast(I32), d_scales[0].bitcast(I32))
         l_n1 = load_list(n1, "l_n1")
         l_n2 = load_list(n2, "l_n2")
         l_n3 = load_list(n3, "l_n3")
@@ -91,35 +114,33 @@ def tile_picked_cdkeynormbdettrim_none_p_kernel(tc, x_words, x_scales, w1, gs, g
         l_n9 = load_list(n9, "l_n9")
         l_n8 = load_list(n8, "l_n8")
 
-        tok_scales = new([P, S], U8, "tok_scales")
-        nc.vector.tensor_copy(tok_scales[:], xs[:].indirect(l_offs[:]))
-        tok_words = new([P, S], U32, "tok_words")
-        nc.vector.tensor_copy(tok_words[:], xw[:].indirect(l_offs[:]))
+        token_scales = new([P, S], U8, "token_scales")
+        nc.vector.tensor_copy(token_scales[:], x_bytes[:].indirect(l_offs[:]))
+        token_words = new([P, S], U32, "token_words")
+        nc.vector.tensor_copy(token_words[:], x_table[:].indirect(l_offs[:]))
+        cand_words_listed = new([P, S], U32, "cand_words_listed")
+        nc.vector.tensor_copy(cand_words_listed[:], x_table[:].indirect(l_cand[:]))
 
-        cand_words_l = new([P, S], U32, "cand_words_l")
-        nc.vector.tensor_copy(cand_words_l[:], xw[:].indirect(l_cand[:]))
-
-        w_bf = after_w([P, PACK, P, PACK], BF16, "w_bf", 0)
+        w_bf = in_head([P, PACK, P, PACK], BF16, "w_bf", 0)
         for q in range(4):
-            src = w_raw[q // 2][:, :, (q % 2) * P:(q % 2 + 1) * P].rearrange("p j (m t) -> p m j t", t=PACK)
+            src = w_raw[q // 2][:, :, block(q % 2)].rearrange("p j (m t) -> p m j t", t=PACK)
             dst = w_bf[:, :, q * 32:(q + 1) * 32, :].rearrange("p t m j -> p m j t")
             if q < 3:
                 nc.scalar.copy(dst, src)
             else:
                 nc.vector.tensor_copy(dst, src)
-        gk_b = in_ring([P, K], "gk_b", 1024)
-        nc.sync.dma_start(gk_b[:], gk.rearrange("k o -> (k o)").partition_broadcast(P))
-        gs_b = in_ring([P, K], "gs_b", 4096)
-        nc.sync.dma_start(gs_b[:], gs.rearrange("k o -> (k o)").partition_broadcast(P))
+        gk_row = in_ring([P, K], "gk_row", GK_ROW_AT)
+        nc.sync.dma_start(gk_row[:], gk.rearrange("k o -> (k o)").partition_broadcast(P))
+        gs_row = in_ring([P, K], "gs_row", GS_ROW_AT)
+        nc.sync.dma_start(gs_row[:], gs.rearrange("k o -> (k o)").partition_broadcast(P))
         w_codes = new([P, S], U32, "w_codes")
         w_scales = new([P, S], U8, "w_scales")
         for t in range(PACK):
-            cols = slice(t * P, (t + 1) * P)
-            nc.vector.quantize_mx(out=w_codes[:, cols].bitcast(FP8X4), scales=w_scales[:, cols], in_=w_bf[:, t].rearrange("p m j -> p (m j)"))
+            nc.vector.quantize_mx(out=w_codes[:, block(t)].bitcast(FP8X4), scales=w_scales[:, block(t)], in_=w_bf[:, t].rearrange("p m j -> p (m j)"))
 
-        def product(acc, t, lw, ls, rw, rs, places=slice(0, S)):
-            cols = slice(t * P, (t + 1) * P)
-            nc.tensor.matmul_mx(out=acc[:, places], lhsT=lw[:, cols].bitcast(FP8X4), lhsT_scale=ls[:, cols], rhs=rw[:, places].bitcast(FP8X4), rhs_scale=rs[:, places], start=True, stop=True)
+        def product(acc, t, still_words, still_scales, moving_words, moving_scales):
+            nc.tensor.matmul_mx(out=acc[:], lhsT=still_words[:, block(t)].bitcast(FP8X4), lhsT_scale=still_scales[:, block(t)],
+                                rhs=moving_words[:].bitcast(FP8X4), rhs_scale=moving_scales[:], start=True, stop=True)
 
         def deal_words(dst, src):
             nc.vector.tensor_copy(dst[:].rearrange("p (t c i) -> p c t i", t=PACK, i=4), src[:].rearrange("p (c i t) -> p c t i", t=PACK, i=4))
@@ -127,163 +148,170 @@ def tile_picked_cdkeynormbdettrim_none_p_kernel(tc, x_words, x_scales, w1, gs, g
         def deal_bytes(dst, src):
             nc.vector.tensor_copy(dst[:].rearrange("p (t m) -> p m t", t=PACK), src[:].rearrange("p (m t) -> p m t", t=PACK))
 
-        def gather(engine, dst, window, offsets, scale=1.0):
-            if engine == "scalar":
-                nc.scalar.activation(dst, window.indirect(offsets), ACT.Copy, scale=scale)
-            else:
-                nc.vector.tensor_copy(dst, window.indirect(offsets))
-
-        def bank(kind, n, name):
-            return psum.tile([P, S], F32, name=name, tag="%s%d" % (kind, n))
-
-        def turned_sum(dst, first, second):
-            nc.tensor.matmul(dst, first, ident[:], start=True, stop=False, is_transpose=True)
-            nc.tensor.matmul(dst, second, ident[:], start=False, stop=True, is_transpose=True)
-
-        def block(n):
-            return slice(n * P, (n + 1) * P)
-
-        def add_turned(banks, t, term, start=False, stop=False):
-            for jb in range(4):
-                nc.tensor.matmul(banks[jb][:, block(t)], term[:, block(jb)], ident[:], start=start, stop=stop, is_transpose=True)
+        def add_block(turned, jb, t, term, start, stop):
+            nc.tensor.matmul(turned[jb][:, block(t)], term[:, block(jb)], ident[:], start=start, stop=stop, is_transpose=True)
 
         def quantise(name, turned, gain):
-            woven = in_ring([P, S, PACK], name + "_bf", 8192, BF16)
+            woven = in_ring([P, S, PACK], name + "_woven", WOVEN_AT, BF16)
             codes = new([P, S], U32, name + "_codes")
             scales = new([P, S], U8, name + "_scales")
-            gain_v = gain[:].rearrange("j (p u e) -> j u p e", u=2, e=2)
+            gain_view = gain[:].rearrange("j (p u e) -> j u p e", u=2, e=2)
             for h in range(2):
                 pairs = bank("A", h, name + "_pairs%d" % h)
-                for b2 in range(2):
-                    jb = 2 * h + b2
-                    flat = in_ring([P, K], name + "_flat3", 13824, BF16) if jb == 3 else new([P, K], BF16, name + "_flat%d" % jb)
-                    nc.vector.tensor_tensor(flat[:].rearrange("j (u p e) -> j u p e", u=2, e=2), turned[jb][:].rearrange("j (u e p) -> j u p e", u=2, e=2), gain_v, ALU.mult)
+                for n in range(2):
+                    jb = 2 * h + n
+                    flat_name = name + "_flat%d" % jb
+                    flat = in_ring([P, K], flat_name, LAST_FLAT_AT, BF16) if jb == BLOCKS - 1 else new([P, K], BF16, flat_name)
+                    nc.vector.tensor_tensor(flat[:].rearrange("j (u p e) -> j u p e", u=2, e=2), turned[jb][:].rearrange("j (u e p) -> j u p e", u=2, e=2), gain_view, ALU.mult)
                     words = flat[:].bitcast(F32)
                     for u in range(2):
-                        nc.tensor.transpose(pairs[:, block(2 * b2 + u)], words[:, block(u)], ident[:])
-                cols = slice(h * HALF, (h + 1) * HALF)
-                dst = woven[:, cols, :].rearrange("p c t -> p (c t)")
-                nc.scalar.copy(dst.bitcast(F32).rearrange("p (b j u) -> p b j u", b=2, u=2), pairs[:].rearrange("p (b u j) -> p b j u", b=2, u=2))
+                        nc.tensor.transpose(pairs[:, block(2 * n + u)], words[:, block(u)], ident[:])
+                dst = woven[:, h * HALF:(h + 1) * HALF, :].rearrange("p c t -> p (c t)")
+                nc.scalar.copy(dst.bitcast(F32).rearrange("p (n j u) -> p n j u", n=2, u=2), pairs[:].rearrange("p (n u j) -> p n j u", n=2, u=2))
             for h in range(2):
                 cols = slice(h * HALF, (h + 1) * HALF)
                 nc.vector.quantize_mx(out=codes[:, cols].bitcast(FP8X4), scales=scales[:, cols], in_=woven[:, cols, :].rearrange("p c t -> p (c t)"))
             return codes, scales
 
-        ys = []
+        y_acc = []
         for t in range(PACK):
-            ys.append(bank("A", t, "y%d" % t))
-            product(ys[t], t, w_codes, w_scales, tok_words, tok_scales)
+            y_acc.append(bank("A", t, "y%d" % t))
+            product(y_acc[t], t, w_codes, w_scales, token_words, token_scales)
 
-        cand_scales_l = after_w([P, S], U8, "cand_scales_l", 2048)
-        nc.vector.tensor_copy(cand_scales_l[:], xs[:].indirect(l_cand[:]))
-        key_scales_l = after_w([P, S], U8, "key_scales_l", 2560)
-        nc.vector.tensor_copy(key_scales_l[:], ds[:].indirect(l_k1[:]))
-        key_words_l = after_w([P, S], U32, "key_words_l", 3072)
-        nc.vector.tensor_copy(key_words_l[:], dw[:].indirect(l_k1[:]))
-        key_scales_d = new([P, S], U8, "key_scales_d")
-        deal_bytes(key_scales_d, key_scales_l)
+        cand_scales_listed = in_head([P, S], U8, "cand_scales_listed", CAND_SCALES_AT)
+        nc.vector.tensor_copy(cand_scales_listed[:], x_bytes[:].indirect(l_cand[:]))
+        key_scales_listed = in_head([P, S], U8, "key_scales_listed", KEY_SCALES_AT)
+        nc.vector.tensor_copy(key_scales_listed[:], d_bytes[:].indirect(l_k1[:]))
+        key_words_listed = in_head([P, S], U32, "key_words_listed", KEY_WORDS_AT)
+        nc.vector.tensor_copy(key_words_listed[:], d_table[:].indirect(l_k1[:]))
+        key_scales_dealt = new([P, S], U8, "key_scales_dealt")
+        deal_bytes(key_scales_dealt, key_scales_listed)
         key_words = new([P, S], U32, "key_words")
-        deal_words(key_words, key_words_l)
-        for e in range(4):
-            first = 8 * e
-            nc.sync.dma_start(key_scales[e:P:32, :].bitcast(I32), key_scales_d[first:P:32, :].bitcast(I32))
+        deal_words(key_words, key_words_listed)
+        for r in range(4):
+            nc.sync.dma_start(key_scales[r:P:32, :].bitcast(I32), key_scales_dealt[8 * r:P:32, :].bitcast(I32))
 
-        turned = [bank("B", jb, "z2_turned%d" % jb) for jb in range(4)]
-        brows = [new([P, 2 * S], F32, "brows%d" % t) for t in range(PACK)]
-        g7 = [brows[t][:, S:] for t in range(PACK)]
-        g5 = [new([P, S], F32, "g5_%d" % t) for t in range(PACK)]
+        turned = [bank("B", jb, "z2_turned%d" % jb) for jb in range(BLOCKS)]
+        b_rows = [new([P, 2 * S], F32, "b_rows%d" % t) for t in range(PACK)]
+        minus7 = [b_rows[t][:, S:] for t in range(PACK)]
+        got5 = [new([P, S], F32, "got5_%d" % t) for t in range(PACK)]
         cut = [new([P, S], F32, "cut%d" % t) for t in range(PACK)]
-        for pair in ((0, 1), (2, 3)):
+        scalar_n5_tiles = [t for t in range(PACK) if t != VECTOR_N5_TILE]
+        tile_pairs = ((0, 1), (2, 3))
+        for pair in tile_pairs:
             for t in pair:
-                nc.scalar.activation(rows[t][:, :S], ys[t][:], ACT.Copy)
+                nc.scalar.activation(rows[t][:, :S], y_acc[t][:], ACT.Copy)
             for t in pair:
-                gather("scalar", g7[t], rows[t][:], l_n7[:], -1.0)
-        for t in (0, 1, 3):
-            gather("scalar", g5[t][:], rows[t][:], l_n5[:])
-        for pair in ((0, 1), (2, 3)):
+                scalar_gather(minus7[t], rows[t][:], l_n7[:], -1.0)
+        for t in scalar_n5_tiles:
+            scalar_gather(got5[t][:], rows[t][:], l_n5[:])
+        for pair in tile_pairs:
             lead = {t: new([P, S], F32, "lead%d" % t) for t in pair}
             for t in pair:
-                nc.vector.tensor_tensor(lead[t][:], rows[t][:].indirect(l_n6[:]), g7[t], ALU.add)
+                nc.vector.tensor_tensor(lead[t][:], rows[t][:].indirect(l_n6[:]), minus7[t], ALU.add)
             for t in pair:
                 nc.vector.tensor_scalar(cut[t][:], lead[t][:], -1.0, 0.0, ALU.mult, ALU.min)
-            if pair[0] == 0:
-                nc.vector.tensor_tensor(g5[2][:], rows[2][:].indirect(l_n5[:]), g7[2], ALU.add)
-        terms = [(t, rows[t][:, :S]) for t in range(PACK)] + [(t, g7[t]) for t in (0, 1, 3)]
-        terms += [(0, cut[0][:]), (1, cut[1][:])] + [(t, g5[t][:]) for t in (2, 0, 1)]
-        for n, (t, term) in enumerate(terms):
-            add_turned(turned, t, term, start=(n == 0))
-        for jb in range(4):
-            for t, term in ((3, g5[3]), (2, cut[2]), (3, cut[3])):
-                nc.tensor.matmul(turned[jb][:, block(t)], term[:, block(jb)], ident[:], start=False, stop=(term is cut[3]), is_transpose=True)
-        cand_words = new([P, S], U32, "cand_words", "lead3")
-        deal_words(cand_words, cand_words_l)
-        cand_scales = new([P, S], U8, "cand_scales", "lead2")
-        deal_bytes(cand_scales, cand_scales_l)
-        z2_codes, z2_scales = quantise("z2", turned, gk_b)
+            if pair == tile_pairs[0]:
+                nc.vector.tensor_tensor(got5[VECTOR_N5_TILE][:], rows[VECTOR_N5_TILE][:].indirect(l_n5[:]), minus7[VECTOR_N5_TILE], ALU.add)
+        early = [(t, rows[t][:, :S]) for t in range(PACK)] + [(t, minus7[t]) for t in scalar_n5_tiles]
+        early += [(t, cut[t][:]) for t in tile_pairs[0]] + [(t, got5[t][:]) for t in [VECTOR_N5_TILE] + scalar_n5_tiles[:-1]]
+        late = [(scalar_n5_tiles[-1], got5[scalar_n5_tiles[-1]][:])] + [(t, cut[t][:]) for t in tile_pairs[1]]
+        for n, (t, term) in enumerate(early):
+            for jb in range(BLOCKS):
+                add_block(turned, jb, t, term, n == 0, False)
+        for jb in range(BLOCKS):
+            for n, (t, term) in enumerate(late):
+                add_block(turned, jb, t, term, False, n == len(late) - 1)
+        cand_words = new([P, S], U32, "cand_words", after="lead3")
+        deal_words(cand_words, cand_words_listed)
+        cand_scales = new([P, S], U8, "cand_scales", after="lead2")
+        deal_bytes(cand_scales, cand_scales_listed)
+        z2_codes, z2_scales = quantise("z2", turned, gk_row)
 
-        b_acc = [bank("A", (t + 2) % 4, "b%d" % t) for t in range(PACK)]
+        b_acc = [bank("A", (t + 2) % PACK, "b%d" % t) for t in range(PACK)]
         for t in range(PACK):
             product(b_acc[t], t, key_words, key_scales, z2_codes, z2_scales)
-        turned = [bank("B", jb, "z_turned%d" % jb) for jb in range(4)]
+
+        def factor_tile(step, name):
+            if step == 0:
+                return new([P, S], F32, name)
+            place = (step - 1) % 3
+            return new([P, S], F32, name, after="z2_flat1") if place == 1 else in_ring([P, S], name, (CHAIN_AT, None, AFTER_FLAT_AT)[place])
+
+        turned = [bank("B", jb, "z_turned%d" % jb) for jb in range(BLOCKS)]
         for t in range(PACK):
-            y = rows[t]
-            for n, (la, lb, factor, nm) in enumerate(((l_n1, l_n2, 0.75, "12"), (l_n3, l_n4, -0.75, "34"))):
-                slot = ("g12_0", 16384, "z2_flat1", 14336, 16384, "z2_flat1", 14336, 16384)[2 * t + n]
-                g = new([P, S], F32, "g%s_%d" % (nm, t), slot) if isinstance(slot, str) else in_ring([P, S], "g%s_%d" % (nm, t), slot)
-                gather("scalar", g[:], y[:], la[:], factor)
-                pr = in_ring([P, S], "p%s_%d" % (nm, t), 2048 * n) if t % 2 == 1 else new([P, S], F32, "p%s_%d" % (nm, t), ("g5_3", "z2_flat2")[n])
-                if (t, n) == (0, 0):
+            for n, (first, second, constant) in enumerate(((l_n1, l_n2, 0.75), (l_n3, l_n4, -0.75))):
+                step = 2 * t + n
+                factor = factor_tile(step, "factor%d" % step)
+                scalar_gather(factor[:], rows[t][:], first[:], constant)
+                term_name = "term%d" % step
+                term = in_ring([P, S], term_name, PRODUCT_AT[n]) if t % 2 == 1 else new([P, S], F32, term_name, after=("got5_3", "z2_flat2")[n])
+                if step == 0:
                     other = new([P, S], F32, "other")
-                    gather("scalar", other[:], y[:], lb[:])
-                    nc.gpsimd.tensor_tensor(pr[:], g[:], other[:], ALU.mult)
+                    scalar_gather(other[:], rows[t][:], second[:])
+                    nc.gpsimd.tensor_tensor(term[:], factor[:], other[:], ALU.mult)
                 else:
-                    nc.vector.tensor_tensor(pr[:], y[:].indirect(lb[:]), g[:], ALU.mult)
-                for jb in range(4):
-                    nc.tensor.matmul(turned[jb][:, block(t)], pr[:, block(jb)], ident[:], start=(n == 0), stop=(n == 1), is_transpose=True)
+                    nc.vector.tensor_tensor(term[:], rows[t][:].indirect(second[:]), factor[:], ALU.mult)
+                for jb in range(BLOCKS):
+                    add_block(turned, jb, t, term, n == 0, n == 1)
 
-        twin, den = {}, {}
-        for t in (2, 0, 1, 3):
-            nc.scalar.activation(brows[t][:, :S], b_acc[t][:], ACT.Abs)
-            if t >= 2:
+        twin, got9, total = {}, {}, {}
+        for t in (FUSED_SUM_TILES[0], 0, 1, FUSED_SUM_TILES[1]):
+            nc.scalar.activation(b_rows[t][:, :S], b_acc[t][:], ACT.Abs)
+            if t in FUSED_SUM_TILES:
                 twin[t] = new([P, S], F32, "twin%d" % t)
-                nc.sync.dma_start(twin[t][:], brows[t][:, :S])
+                nc.sync.dma_start(twin[t][:], b_rows[t][:, :S])
             else:
-                g9 = new([P, S], F32, "g9_%d" % t)
-                gather("scalar", g9[:], brows[t][:], l_n9[:])
-                den[t] = in_ring([P, S], "den0", 16384) if t == 0 else new([P, S], F32, "den1")
-                nc.gpsimd.tensor_tensor(den[t][:], brows[t][:, :S], g9[:], ALU.add)
-        z_codes, z_scales = quantise("z", turned, gs_b)
-        for t, offset in ((2, 4096), (3, 8192)):
-            den[t] = in_ring([P, S], "den%d" % t, offset)
-            nc.vector.tensor_tensor(den[t][:], brows[t][:].indirect(l_n9[:]), twin[t][:], ALU.add)
+                got9[t] = new([P, S], F32, "got9_%d" % t)
+                scalar_gather(got9[t][:], b_rows[t][:], l_n9[:])
+                if t == 0:
+                    total[t] = in_ring([P, S], "total0", CHAIN_AT)
+                    nc.gpsimd.tensor_tensor(total[t][:], b_rows[t][:, :S], got9[t][:], ALU.add)
+        z_codes, z_scales = quantise("z", turned, gs_row)
+        total[1] = in_ring([P, S], "total1", SUM_AT[0])
+        nc.vector.tensor_tensor(total[1][:], b_rows[1][:, :S], got9[1][:], ALU.add)
+        for t, offset in zip(FUSED_SUM_TILES, (SUM_AT[1], WOVEN_AT)):
+            total[t] = in_ring([P, S], "total%d" % t, offset)
+            nc.vector.tensor_tensor(total[t][:], b_rows[t][:].indirect(l_n9[:]), twin[t][:], ALU.add)
 
-        def inverse(t):
-            root = new([P, S], F32, "root%d" % t) if t != 2 else in_ring([P, S], "root2", 12288)
-            nc.scalar.activation(root[:], den[t][:], ACT.Abs_reciprocal_sqrt, bias=eight[:])
-            if t < 2:
-                inv_t = new([P, S], F32, "inv_t%d" % t)
-                nc.scalar.activation(inv_t[:], root[:], ACT.Square)
-            else:
-                inv_t = new([P, S], F32, "inv_t2", "twin3") if t == 2 else in_ring([P, S], "inv_t3", 12288)
-                nc.gpsimd.tensor_tensor(inv_t[:], root[:], root[:], ALU.mult)
-            return inv_t
+        root = {}
+
+        def inverse_root(t, tile):
+            root[t] = tile
+            nc.scalar.activation(tile[:], total[t][:], ACT.Abs_reciprocal_sqrt, bias=eight[:])
+
+        inverse_root(0, new([P, S], F32, "root0"))
+        inverse_root(1, in_ring([P, S], "root1", AFTER_FLAT_AT))
+        inverse_root(2, in_ring([P, S], "root2", CHAIN_AT))
+        inverse = [in_ring([P, S], "inverse0", BEFORE_FLAT_AT), new([P, S], F32, "inverse1", after="twin3"),
+                   in_ring([P, S], "inverse2", AFTER_FLAT_AT), in_ring([P, S], "inverse3", CHAIN_AT)]
+        nc.scalar.activation(inverse[0][:], root[0][:], ACT.Square)
 
         out_rows = out.rearrange("(p t) n -> t p n", t=PACK)
-        inv_t = [inverse(t) for t in range(PACK - 1)]
-        accs = [bank("B", t, "a%d" % t) for t in range(PACK)]
+        a_acc = [bank("B", t, "a%d" % t) for t in range(PACK)]
         for t in range(PACK):
-            product(accs[t], t, cand_words, cand_scales, z_codes, z_scales)
-        nc.scalar.activation(rows[0][:, :S], accs[0][:], ACT.Copy)
-        nc.vector.tensor_copy(rows[1][:, :S], accs[1][:])
-        inv_t.append(inverse(PACK - 1))
+            product(a_acc[t], t, cand_words, cand_scales, z_codes, z_scales)
+        nc.scalar.activation(rows[0][:, :S], a_acc[0][:], ACT.Copy)
+        nc.vector.tensor_copy(rows[1][:, :S], a_acc[1][:])
+        last = PACK - 1
+        inverse_root(last, new([P, S], F32, "root3"))
+        for t in range(1, last):
+            nc.gpsimd.tensor_tensor(inverse[t][:], root[t][:], root[t][:], ALU.mult)
+        whole = [(slice(0, S), slice(0, LIST_COLS))]
+        halves = [(slice(h * HALF, (h + 1) * HALF), slice(h * LIST_COLS // 2, (h + 1) * LIST_COLS // 2)) for h in range(2)]
         for t in range(PACK):
             if t > 1:
-                nc.scalar.activation(rows[t][:, :S], accs[t][:], ACT.Copy)
-            g8 = new([P, S], F32, "g8_%d" % t)
-            num = new([P, S], F32, "num%d" % t)
-            res = new([P, S], F32, "res%d" % t)
-            for cols, lc in (halves() if t == PACK - 1 else [(slice(0, S), slice(0, LCOLS))]):
-                gather("scalar" if t > 0 else "vector", g8[:, cols], rows[t][:], l_n8[:, lc])
-                nc.vector.tensor_tensor(num[:, cols], accs[t][:, cols], g8[:, cols], ALU.subtract)
-                nc.vector.tensor_tensor(res[:, cols], inv_t[t][:, cols], num[:, cols], ALU.mult)
-                nc.sync.dma_start(out_rows[t][:, cols], res[:, cols])
+                nc.scalar.activation(rows[t][:, :S], a_acc[t][:], ACT.Copy)
+            if t == last:
+                nc.scalar.activation(inverse[t][:], root[t][:], ACT.Square)
+            got8 = new([P, S], F32, "got8_%d" % t)
+            upper = new([P, S], F32, "upper%d" % t)
+            result = new([P, S], F32, "result%d" % t)
+            for cols, list_cols in (halves if t == last else whole):
+                if t == 0:
+                    nc.vector.tensor_copy(got8[:, cols], rows[t][:].indirect(l_n8[:, list_cols]))
+                else:
+                    scalar_gather(got8[:, cols], rows[t][:], l_n8[:, list_cols])
+                nc.vector.tensor_tensor(upper[:, cols], a_acc[t][:, cols], got8[:, cols], ALU.subtract)
+                nc.vector.tensor_tensor(result[:, cols], inverse[t][:, cols], upper[:, cols], ALU.mult)
+                nc.sync.dma_start(out_rows[t][:, cols], result[:, cols])

from contextlib import ExitStack

import concourse.mybir as mybir
from concourse.masks import make_identity

K, T, S, G = 512, 1024, 512, 2048
FLOPS = 3 * 2 * 512 * 512 * 512

F32 = mybir.dt.float32
BF16 = mybir.dt.bfloat16
I32 = mybir.dt.int32
U32 = mybir.dt.uint32
U16 = mybir.dt.uint16
U8 = mybir.dt.uint8
FP8X4 = mybir.dt.float8_e4m3fn_x4
ALU = mybir.AluOpType
ACT = mybir.ActivationFunctionType

P = 128
PACK = 4
BLOCKS = S // P
HALF = S // 2
LIST_COLS = S // 16
TILE_BYTES = 4 * S

W_RAW_AT = (0, 2 * TILE_BYTES)
GK_ROW_AT = TILE_BYTES // 2
GS_ROW_AT = 2 * TILE_BYTES
PRODUCT_AT = (0, TILE_BYTES)
SUM_AT = (GS_ROW_AT - TILE_BYTES // 2, GS_ROW_AT + TILE_BYTES // 2)
WOVEN_AT = 4 * TILE_BYTES
BEFORE_FLAT_AT = 6 * TILE_BYTES
LAST_FLAT_AT = 7 * TILE_BYTES - TILE_BYTES // 4
AFTER_FLAT_AT = 7 * TILE_BYTES
CHAIN_AT = 8 * TILE_BYTES

CAND_SCALES_AT, KEY_SCALES_AT, KEY_WORDS_AT = TILE_BYTES, TILE_BYTES + S, TILE_BYTES + 2 * S

VECTOR_N5_TILE = 2
FUSED_SUM_TILES = (2, 3)


def tile_picked_cdkeynormbdettrim_none_p_kernel(tc, x_words, x_scales, w1, gs, gk, d_words, d_scales, offs, n1, n2, n3, n4, n5, n6, n7, cand, k1, n8, n9, out):
    nc = tc.nc
    with ExitStack() as ctx:
        lists = ctx.enter_context(tc.tile_pool(name="lists", bufs=1))
        sb = ctx.enter_context(tc.tile_pool(name="sb", bufs=1))
        head = ctx.enter_context(tc.tile_pool(name="head", bufs=1))
        ring = ctx.enter_context(tc.tile_pool(name="ring", bufs=1))
        psum = ctx.enter_context(tc.psum_pool(name="psum", bufs=1))

        def new(shape, dtype, name, after=None):
            return sb.tile(shape, dtype, name=name, tag=after or name, align_bytes=64)

        def in_head(shape, dtype, name, offset):
            return head.tile(shape, dtype, name=name, align_bytes=64, offset=offset)

        def in_ring(shape, name, offset, dtype=F32):
            return ring.tile(shape, dtype, name=name, align_bytes=64, offset=offset)

        def bank(kind, n, name):
            return psum.tile([P, S], F32, name=name, tag="%s%d" % (kind, n))

        def block(n):
            return slice(n * P, (n + 1) * P)

        def load_list(src, name):
            tile = lists.tile([P, LIST_COLS], U16, name=name)
            nc.sync.dma_start(tile[:], src)
            return tile

        def scalar_gather(dst, window, offsets, scale=1.0):
            nc.scalar.activation(dst, window.indirect(offsets), ACT.Copy, scale=scale)

        x_bytes = new([P, T], U8, "x_bytes")
        nc.gpsimd.memset(x_bytes[:].bitcast(I32), 0)
        eight = new([P, 1], F32, "eight")
        nc.gpsimd.memset(eight[:], 8.0)
        d_bytes = new([P, G], U8, "d_bytes")
        nc.gpsimd.memset(d_bytes[:].bitcast(I32), 0)
        key_scales = new([P, S], U8, "key_scales")
        nc.gpsimd.memset(key_scales[:].bitcast(I32), 0)
        warm = new([P, 1], F32, "warm")
        nc.scalar.activation(warm[:], eight[:], ACT.Abs_reciprocal_sqrt, bias=eight[:])
        ident = new([P, P], F32, "ident")
        make_identity(nc, ident[:])
        rows = [new([P, 2 * S], F32, "rows%d" % t) for t in range(PACK)]
        for t in range(PACK):
            nc.vector.memset(rows[t][:, S:], 0.0)

        l_offs = load_list(offs, "l_offs")
        x_scale_rows = x_scales[0].bitcast(I32)
        for r in range(4):
            nc.sync.dma_start(x_bytes[r:P:32, :].bitcast(I32), x_scale_rows[r:16:4, :])
        x_table = new([P, T], U32, "x_table")
        nc.sync.dma_start(x_table[:].bitcast(I32), x_words[0].rearrange("p n t -> p (n t)").bitcast(I32))
        l_cand = load_list(cand, "l_cand")
        w_rows = w1.rearrange("(p j) c -> p j c", j=PACK)
        w_raw = []
        for h in range(2):
            w_raw.append(in_ring([P, PACK, HALF], "w_raw%d" % h, W_RAW_AT[h]))
            nc.sync.dma_start(w_raw[h][:], w_rows[:, :, h * HALF:(h + 1) * HALF])
        l_n7 = load_list(n7, "l_n7")
        l_n5 = load_list(n5, "l_n5")
        l_n6 = load_list(n6, "l_n6")
        d_table = new([P, G], U32, "d_table")
        nc.sync.dma_start(d_table[:].bitcast(I32), d_words[0].rearrange("p n t -> p (n t)").bitcast(I32))
        l_k1 = load_list(k1, "l_k1")
        nc.sync.dma_start(d_bytes[0:P:8, :].bitcast(I32), d_scales[0].bitcast(I32))
        l_n1 = load_list(n1, "l_n1")
        l_n2 = load_list(n2, "l_n2")
        l_n3 = load_list(n3, "l_n3")
        l_n4 = load_list(n4, "l_n4")
        l_n9 = load_list(n9, "l_n9")
        l_n8 = load_list(n8, "l_n8")

        token_scales = new([P, S], U8, "token_scales")
        nc.vector.tensor_copy(token_scales[:], x_bytes[:].indirect(l_offs[:]))
        token_words = new([P, S], U32, "token_words")
        nc.vector.tensor_copy(token_words[:], x_table[:].indirect(l_offs[:]))
        cand_words_listed = new([P, S], U32, "cand_words_listed")
        nc.vector.tensor_copy(cand_words_listed[:], x_table[:].indirect(l_cand[:]))

        w_bf = in_head([P, PACK, P, PACK], BF16, "w_bf", 0)
        for q in range(4):
            src = w_raw[q // 2][:, :, block(q % 2)].rearrange("p j (m t) -> p m j t", t=PACK)
            dst = w_bf[:, :, q * 32:(q + 1) * 32, :].rearrange("p t m j -> p m j t")
            if q < 3:
                nc.scalar.copy(dst, src)
            else:
                nc.vector.tensor_copy(dst, src)
        gk_row = in_ring([P, K], "gk_row", GK_ROW_AT)
        nc.sync.dma_start(gk_row[:], gk.rearrange("k o -> (k o)").partition_broadcast(P))
        gs_row = in_ring([P, K], "gs_row", GS_ROW_AT)
        nc.sync.dma_start(gs_row[:], gs.rearrange("k o -> (k o)").partition_broadcast(P))
        w_codes = new([P, S], U32, "w_codes")
        w_scales = new([P, S], U8, "w_scales")
        for t in range(PACK):
            nc.vector.quantize_mx(out=w_codes[:, block(t)].bitcast(FP8X4), scales=w_scales[:, block(t)], in_=w_bf[:, t].rearrange("p m j -> p (m j)"))

        def product(acc, t, still_words, still_scales, moving_words, moving_scales):
            nc.tensor.matmul_mx(out=acc[:], lhsT=still_words[:, block(t)].bitcast(FP8X4), lhsT_scale=still_scales[:, block(t)],
                                rhs=moving_words[:].bitcast(FP8X4), rhs_scale=moving_scales[:], start=True, stop=True)

        def deal_words(dst, src):
            nc.vector.tensor_copy(dst[:].rearrange("p (t c i) -> p c t i", t=PACK, i=4), src[:].rearrange("p (c i t) -> p c t i", t=PACK, i=4))

        def deal_bytes(dst, src):
            nc.vector.tensor_copy(dst[:].rearrange("p (t m) -> p m t", t=PACK), src[:].rearrange("p (m t) -> p m t", t=PACK))

        def add_block(turned, jb, t, term, start, stop):
            nc.tensor.matmul(turned[jb][:, block(t)], term[:, block(jb)], ident[:], start=start, stop=stop, is_transpose=True)

        def quantise(name, turned, gain):
            woven = in_ring([P, S, PACK], name + "_woven", WOVEN_AT, BF16)
            codes = new([P, S], U32, name + "_codes")
            scales = new([P, S], U8, name + "_scales")
            gain_view = gain[:].rearrange("j (p u e) -> j u p e", u=2, e=2)
            for h in range(2):
                pairs = bank("A", h, name + "_pairs%d" % h)
                for n in range(2):
                    jb = 2 * h + n
                    flat_name = name + "_flat%d" % jb
                    flat = in_ring([P, K], flat_name, LAST_FLAT_AT, BF16) if jb == BLOCKS - 1 else new([P, K], BF16, flat_name)
                    nc.vector.tensor_tensor(flat[:].rearrange("j (u p e) -> j u p e", u=2, e=2), turned[jb][:].rearrange("j (u e p) -> j u p e", u=2, e=2), gain_view, ALU.mult)
                    words = flat[:].bitcast(F32)
                    for u in range(2):
                        nc.tensor.transpose(pairs[:, block(2 * n + u)], words[:, block(u)], ident[:])
                dst = woven[:, h * HALF:(h + 1) * HALF, :].rearrange("p c t -> p (c t)")
                nc.scalar.copy(dst.bitcast(F32).rearrange("p (n j u) -> p n j u", n=2, u=2), pairs[:].rearrange("p (n u j) -> p n j u", n=2, u=2))
            for h in range(2):
                cols = slice(h * HALF, (h + 1) * HALF)
                nc.vector.quantize_mx(out=codes[:, cols].bitcast(FP8X4), scales=scales[:, cols], in_=woven[:, cols, :].rearrange("p c t -> p (c t)"))
            return codes, scales

        y_acc = []
        for t in range(PACK):
            y_acc.append(bank("A", t, "y%d" % t))
            product(y_acc[t], t, w_codes, w_scales, token_words, token_scales)

        cand_scales_listed = in_head([P, S], U8, "cand_scales_listed", CAND_SCALES_AT)
        nc.vector.tensor_copy(cand_scales_listed[:], x_bytes[:].indirect(l_cand[:]))
        key_scales_listed = in_head([P, S], U8, "key_scales_listed", KEY_SCALES_AT)
        nc.vector.tensor_copy(key_scales_listed[:], d_bytes[:].indirect(l_k1[:]))
        key_words_listed = in_head([P, S], U32, "key_words_listed", KEY_WORDS_AT)
        nc.vector.tensor_copy(key_words_listed[:], d_table[:].indirect(l_k1[:]))
        key_scales_dealt = new([P, S], U8, "key_scales_dealt")
        deal_bytes(key_scales_dealt, key_scales_listed)
        key_words = new([P, S], U32, "key_words")
        deal_words(key_words, key_words_listed)
        for r in range(4):
            nc.sync.dma_start(key_scales[r:P:32, :].bitcast(I32), key_scales_dealt[8 * r:P:32, :].bitcast(I32))

        turned = [bank("B", jb, "z2_turned%d" % jb) for jb in range(BLOCKS)]
        b_rows = [new([P, 2 * S], F32, "b_rows%d" % t) for t in range(PACK)]
        minus7 = [b_rows[t][:, S:] for t in range(PACK)]
        got5 = [new([P, S], F32, "got5_%d" % t) for t in range(PACK)]
        cut = [new([P, S], F32, "cut%d" % t) for t in range(PACK)]
        scalar_n5_tiles = [t for t in range(PACK) if t != VECTOR_N5_TILE]
        tile_pairs = ((0, 1), (2, 3))
        for pair in tile_pairs:
            for t in pair:
                nc.scalar.activation(rows[t][:, :S], y_acc[t][:], ACT.Copy)
            for t in pair:
                scalar_gather(minus7[t], rows[t][:], l_n7[:], -1.0)
        for t in scalar_n5_tiles:
            scalar_gather(got5[t][:], rows[t][:], l_n5[:])
        for pair in tile_pairs:
            lead = {t: new([P, S], F32, "lead%d" % t) for t in pair}
            for t in pair:
                nc.vector.tensor_tensor(lead[t][:], rows[t][:].indirect(l_n6[:]), minus7[t], ALU.add)
            for t in pair:
                nc.vector.tensor_scalar(cut[t][:], lead[t][:], -1.0, 0.0, ALU.mult, ALU.min)
            if pair == tile_pairs[0]:
                nc.vector.tensor_tensor(got5[VECTOR_N5_TILE][:], rows[VECTOR_N5_TILE][:].indirect(l_n5[:]), minus7[VECTOR_N5_TILE], ALU.add)
        early = [(t, rows[t][:, :S]) for t in range(PACK)] + [(t, minus7[t]) for t in scalar_n5_tiles]
        early += [(t, cut[t][:]) for t in tile_pairs[0]] + [(t, got5[t][:]) for t in [VECTOR_N5_TILE] + scalar_n5_tiles[:-1]]
        late = [(scalar_n5_tiles[-1], got5[scalar_n5_tiles[-1]][:])] + [(t, cut[t][:]) for t in tile_pairs[1]]
        for n, (t, term) in enumerate(early):
            for jb in range(BLOCKS):
                add_block(turned, jb, t, term, n == 0, False)
        for jb in range(BLOCKS):
            for n, (t, term) in enumerate(late):
                add_block(turned, jb, t, term, False, n == len(late) - 1)
        cand_words = new([P, S], U32, "cand_words", after="lead3")
        deal_words(cand_words, cand_words_listed)
        cand_scales = new([P, S], U8, "cand_scales", after="lead2")
        deal_bytes(cand_scales, cand_scales_listed)
        z2_codes, z2_scales = quantise("z2", turned, gk_row)

        b_acc = [bank("A", (t + 2) % PACK, "b%d" % t) for t in range(PACK)]
        for t in range(PACK):
            product(b_acc[t], t, key_words, key_scales, z2_codes, z2_scales)

        def factor_tile(step, name):
            if step == 0:
                return new([P, S], F32, name)
            place = (step - 1) % 3
            return new([P, S], F32, name, after="z2_flat1") if place == 1 else in_ring([P, S], name, (CHAIN_AT, None, AFTER_FLAT_AT)[place])

        turned = [bank("B", jb, "z_turned%d" % jb) for jb in range(BLOCKS)]
        for t in range(PACK):
            for n, (first, second, constant) in enumerate(((l_n1, l_n2, 0.75), (l_n3, l_n4, -0.75))):
                step = 2 * t + n
                factor = factor_tile(step, "factor%d" % step)
                scalar_gather(factor[:], rows[t][:], first[:], constant)
                term_name = "term%d" % step
                term = in_ring([P, S], term_name, PRODUCT_AT[n]) if t % 2 == 1 else new([P, S], F32, term_name, after=("got5_3", "z2_flat2")[n])
                if step == 0:
                    other = new([P, S], F32, "other")
                    scalar_gather(other[:], rows[t][:], second[:])
                    nc.gpsimd.tensor_tensor(term[:], factor[:], other[:], ALU.mult)
                else:
                    nc.vector.tensor_tensor(term[:], rows[t][:].indirect(second[:]), factor[:], ALU.mult)
                for jb in range(BLOCKS):
                    add_block(turned, jb, t, term, n == 0, n == 1)

        twin, got9, total = {}, {}, {}
        for t in (FUSED_SUM_TILES[0], 0, 1, FUSED_SUM_TILES[1]):
            nc.scalar.activation(b_rows[t][:, :S], b_acc[t][:], ACT.Abs)
            if t in FUSED_SUM_TILES:
                twin[t] = new([P, S], F32, "twin%d" % t)
                nc.sync.dma_start(twin[t][:], b_rows[t][:, :S])
            else:
                got9[t] = new([P, S], F32, "got9_%d" % t)
                scalar_gather(got9[t][:], b_rows[t][:], l_n9[:])
                if t == 0:
                    total[t] = in_ring([P, S], "total0", CHAIN_AT)
                    nc.gpsimd.tensor_tensor(total[t][:], b_rows[t][:, :S], got9[t][:], ALU.add)
        z_codes, z_scales = quantise("z", turned, gs_row)
        total[1] = in_ring([P, S], "total1", SUM_AT[0])
        nc.vector.tensor_tensor(total[1][:], b_rows[1][:, :S], got9[1][:], ALU.add)
        for t, offset in zip(FUSED_SUM_TILES, (SUM_AT[1], WOVEN_AT)):
            total[t] = in_ring([P, S], "total%d" % t, offset)
            nc.vector.tensor_tensor(total[t][:], b_rows[t][:].indirect(l_n9[:]), twin[t][:], ALU.add)

        root = {}

        def inverse_root(t, tile):
            root[t] = tile
            nc.scalar.activation(tile[:], total[t][:], ACT.Abs_reciprocal_sqrt, bias=eight[:])

        inverse_root(0, new([P, S], F32, "root0"))
        inverse_root(1, in_ring([P, S], "root1", AFTER_FLAT_AT))
        inverse_root(2, in_ring([P, S], "root2", CHAIN_AT))
        inverse = [in_ring([P, S], "inverse0", BEFORE_FLAT_AT), new([P, S], F32, "inverse1", after="twin3"),
                   in_ring([P, S], "inverse2", AFTER_FLAT_AT), in_ring([P, S], "inverse3", CHAIN_AT)]
        nc.scalar.activation(inverse[0][:], root[0][:], ACT.Square)

        out_rows = out.rearrange("(p t) n -> t p n", t=PACK)
        a_acc = [bank("B", t, "a%d" % t) for t in range(PACK)]
        for t in range(PACK):
            product(a_acc[t], t, cand_words, cand_scales, z_codes, z_scales)
        nc.scalar.activation(rows[0][:, :S], a_acc[0][:], ACT.Copy)
        nc.vector.tensor_copy(rows[1][:, :S], a_acc[1][:])
        last = PACK - 1
        inverse_root(last, new([P, S], F32, "root3"))
        for t in range(1, last):
            nc.gpsimd.tensor_tensor(inverse[t][:], root[t][:], root[t][:], ALU.mult)
        whole = [(slice(0, S), slice(0, LIST_COLS))]
        halves = [(slice(h * HALF, (h + 1) * HALF), slice(h * LIST_COLS // 2, (h + 1) * LIST_COLS // 2)) for h in range(2)]
        for t in range(PACK):
            if t > 1:
                nc.scalar.activation(rows[t][:, :S], a_acc[t][:], ACT.Copy)
            if t == last:
                nc.scalar.activation(inverse[t][:], root[t][:], ACT.Square)
            got8 = new([P, S], F32, "got8_%d" % t)
            upper = new([P, S], F32, "upper%d" % t)
            result = new([P, S], F32, "result%d" % t)
            for cols, list_cols in (halves if t == last else whole):
                if t == 0:
                    nc.vector.tensor_copy(got8[:, cols], rows[t][:].indirect(l_n8[:, list_cols]))
                else:
                    scalar_gather(got8[:, cols], rows[t][:], l_n8[:, list_cols])
                nc.vector.tensor_tensor(upper[:, cols], a_acc[t][:, cols], got8[:, cols], ALU.subtract)
                nc.vector.tensor_tensor(result[:, cols], inverse[t][:, cols], upper[:, cols], ALU.mult)
                nc.sync.dma_start(out_rows[t][:, cols], result[:, cols])
